import numpy as np, ml_dtypes
CORES = [40,64,80,88,96,104,120,144]
N = 8
import mx_ref
BF = ml_dtypes.bfloat16
def gcols(t, e):
    v = np.concatenate([t.reshape(8, 16, -1, 4), np.zeros((8, 16, 1, 4), BF)], axis=2)
    return np.ascontiguousarray(np.stack([v[g][:, e[g]] for g in range(8)])).reshape(128, -1)
def tile(rs):
    return np.stack(rs, axis=2).reshape(128, -1).astype(BF)
def pick(q, e):
    c = np.concatenate([q[0].reshape(128, -1, 4), np.zeros((128, 1, 4), np.uint8)], axis=1); s = np.concatenate([q[1], np.ones((16, 1), np.uint8)], axis=1)
    return (np.ascontiguousarray(c[:, e].reshape(128, -1)), np.ascontiguousarray(s[:, e]))
def join(*qs):
    return (np.concatenate([q[0] for q in qs], axis=1), np.concatenate([q[1] for q in qs], axis=1))
def put(q, e, v):
    c, s = q[0].reshape(128, -1, 4).copy(), q[1].copy(); c[:, e] = v[0].reshape(128, -1, 4); s[:, e] = v[1]
    return (c.reshape(128, -1), s)
def pk(c, s):
    return (np.ascontiguousarray(c), mx_ref.live(s))
def emit(q):
    return q[0], q[1]
def packed(v, rng):
    q = [mx_ref.quantize(np.ascontiguousarray(v[r])) for r in range(N)]
    return np.stack([a for a, b in q]), np.stack([mx_ref.plane(b, rng) for a, b in q])
def values_of_codes():
    e, c = np.zeros((128, 128, 4), np.float32), np.zeros((128, 2, 4), np.uint8)
    e[np.arange(128), np.arange(128), 0] = 1
    c[:127, :, 0] = np.arange(256).reshape(2, 128).T[:127]
    return mx_ref.matmul(mx_ref.quantize(e.reshape(128, 512).astype(BF)), (c.reshape(128, 8), np.full((16, 2), 127, np.uint8))).T.reshape(-1).astype(np.float64)
CODE_VALUE, SCALE_VALUE = values_of_codes(), 2.0 ** (np.arange(256) - 127.0)
def decode(q):
    return (CODE_VALUE[q[0]].reshape(16, 8, -1, 4) * SCALE_VALUE[q[1]][:, None, :, None] + 0.0).reshape(128, -1).astype(np.float32)
def f(rng, *shape):
    return mx_ref.flush((rng.standard_normal(shape, dtype=np.float32) * np.exp2(rng.integers(-2, 3, shape[:-1] + (1,)))).astype(BF))
def wide(rng, *shape, cols=0):
    v = rng.standard_normal(shape, dtype=np.float32) * np.exp2(rng.integers(-12, 13, shape)).astype(np.float32)
    if cols: v *= np.repeat(np.exp2(rng.integers(-cols, cols + 1, shape[:-2] + (1, shape[-1] // 4))) * (rng.random(shape[:-2] + (1, shape[-1] // 4)) > 0.0625), 4, axis=-1).astype(np.float32)
    return mx_ref.flush(v.astype(BF))
C, R = 256, 3
STEP = [1, 2, 4]
def units(s, way):
    p = s[::16] + np.float32(0.0)
    n = 1 + (s[1::16] > 0) + (s[2::16] > 0) + (s[3::16] > 0)
    o = np.argsort(np.float32(way) * p, axis=1, kind="stable")
    return [np.repeat(o[g], n[g][o[g]]) for g in range(8)]
def segments(bids, asks):
    e, first = np.zeros((2, 8, C), np.int64), np.full((2, 8, C), -1)
    for g in range(8):
        m = min(len(bids[g]), len(asks[g]))
        a = np.stack([bids[g][:m], asks[g][:m]])
        new = np.concatenate([[True], (a[:, 1:] != a[:, :-1]).any(axis=0)])
        e[:, g] = a[:, np.flatnonzero(new)[:C]]
        for i in range(2):
            c, k = np.unique(e[i, g], return_index=True)
            first[i, g, c] = k
    return e, first
def numbers_of(rng):
    return {"x": np.array(f(rng, N, 128, 4 * C)), "u": np.stack([f(rng, 128, 512)] * N), "v": np.array(f(rng, N, 128, 512))}
def common(w, rng):
    c, p = packed(np.stack([w] * N), rng)
    return {"wc": c, "ws": p}
def planted(rng, s, n, less=()):
    d = numbers_of(rng)
    kind = rng.permutation(8) % 3
    sign = np.stack([rng.permutation(8) % 2 * 2.0 - 1.0 for r in range(N)])
    k = np.where(kind > 0, 2.0 ** -30, 1.0)
    x = d["x"].astype(np.float32).reshape(N, 8, 16, C, 4)
    e = ((s[..., None] >> np.arange(8)) & 1) * np.exp2(np.arange(8) - 23.0)
    e = e * np.where(kind == 2, sign * 2.0 ** -7, 1.0)[:, :, None, None] + 0.0
    one = np.repeat(np.where(kind < 2, sign, 0.0)[:, :, None], C, axis=2)
    for r in range(N):
        for g in rng.permutation(8)[:4]: one[r, g, rng.integers(C)] = sign[r, g] * 2.0 ** 30
    price = one + np.sum(e, axis=3)
    for r, g in less:
        n[r, g, np.argmin(price[r, g]) if r % 2 else np.argmax(price[r, g])] = 2
    q = np.where(np.argsort(rng.random((N, 8, C, 3)), axis=3) < n[..., None] - 1, 1, -rng.integers(0, 2, (N, 8, C, 3)))
    x[:, :, 0] = 0
    x[:, :, 0, :, 0] = one
    x[:, :, 8] = e[..., :4]
    x[:, :, 9] = e[..., 4:]
    x[:, :, 10] = 0
    x[:, :, 10, :, :3] = q * np.where(kind == 2, 2.0 ** -30, 2.0 ** -20)[:, None, None]
    x[:, :, 11:] = rng.integers(4, 8, (N, 8, 5, C, 4)) * rng.choice([-1.0, 1.0], (N, 8, 5, C, 4)) * 2.0 ** -20
    u = d["u"][0].astype(np.float32).reshape(128, 128, 4)
    for g in range(8):
        h = 16 * g
        u[:, h:h + 4] = 0
        u[h, h, 0] = k[g]
        u[h + 8:h + 10, h] = k[g]
        for i in range(3): u[h + 10, h + 1 + i, i] = k[g]
    w = np.array(f(rng, 128, 2048)).reshape(128, 4, 8, 16, 4)
    w[::16] = 0
    w[:, :, :, 0] = 0
    w[:, :, :, 8:] = 0
    return {"x": x.reshape(N, 128, 4 * C).astype(BF), "u": np.stack([u.reshape(128, 512).astype(BF)] * N), "v": d["v"], **common(w.reshape(128, 2048), rng)}
def pairs_of(rng):
    return np.argsort(rng.random((N, 8, C)), axis=2) // 2
def setup_inputs(rng):
    return {**numbers_of(rng), **common(f(rng, 128, 2048), rng)}
def setup_inputs_ties(rng):
    d = numbers_of(rng)
    o = rng.permutation(N)
    x = d["x"].reshape(N, 8, 16, C, 4)
    for r in range(N):
        k = np.zeros(C, int) if r == o[0] else rng.permutation(C) % 3
        a = x[r][:, :8, :3].copy()
        a[:, :, 2] = 0
        x[r][:, :8] = a[:, :, k]
    x[o[1]] = 0
    u = d["u"].reshape(N, 8, 16, 128, 4)
    u[:, :, 8:, ::16] = 0
    w = np.array(f(rng, 128, 2048)).reshape(128, 4, 8, 16, 4)
    w[:, :, :, :8] = 0
    return {"x": x.reshape(N, 128, 4 * C), "u": u.reshape(N, 128, 512), "v": d["v"], **common(w.reshape(128, 2048), rng)}
def setup_inputs_near(rng):
    return planted(rng, pairs_of(rng), rng.integers(1, 5, (N, 8, C)))
def setup_inputs_lots(rng):
    n = np.zeros((N, 8, C), np.int64)
    p = rng.permutation(N // 2)
    h = rng.permutation(8) % 2
    less = []
    for i in range(N // 2):
        c = (p[i] + N // 2 * h) % 4
        k = np.array([(1, 4), (2, 3), (4, 4), (1, 1)])[c]
        j = int(rng.integers(2))
        n[2 * i], n[2 * i + 1] = k[:, j, None], k[:, 1 - j, None]
        g = rng.permutation(np.flatnonzero(c == 2))
        less += [(2 * i, int(a)) for a in g[::4]] + [(2 * i + 1, int(a)) for a in g[1::4]]
    return planted(rng, pairs_of(rng), n, less)
def setup_inputs_huge(rng):
    d = numbers_of(rng)
    x = 2.0 ** 30 * (0.6 + 0.2 * rng.random((N, 128, C, 4)))
    c = np.stack([rng.permutation(C) % 2 * 2.0 - 1.0 for r in range(N)])
    o = rng.permutation(N)
    c[o < N // 2] = 1
    c[o == 0] = -1
    x *= c[:, None, :, None]
    u = d["u"][0].astype(np.float32).reshape(128, 128, 4)
    u[:, ::16] = 2.0 ** 30 * (1 - 0.25 * rng.random((128, 8, 4))) * (rng.permutation(8) % 2 * 2.0 - 1.0)[None, :, None]
    w = np.zeros((128, 4, 128, 4), np.float32)
    i = np.arange(128)
    for b in range(4): w[i, b, i, b] = 1
    return {"x": x.astype(np.float32).reshape(N, 128, 4 * C).astype(BF), "u": np.stack([u.reshape(128, 512).astype(BF)] * N), "v": d["v"], **common(w.reshape(128, 2048).astype(BF), rng)}
def setup_inputs_spread(rng):
    d = setup_inputs(rng)
    d["x"] = wide(rng, N, 128, 4 * C, cols=6)
    return d
def check_inputs(d):
    b = []
    for k in ("x", "u", "v"):
        a = np.abs(d[k].astype(np.float32))
        if not (np.isfinite(a).all() and ((a == 0) | (a >= 2.0 ** -30) & (a <= 2.0 ** 30)).all()): b.append("a value of " + k)
    a = d["u"].astype(np.float32)
    if (a != a[:1]).any(): b.append("u differs between ranks")
    if (d["wc"] != d["wc"][:1]).any(): b.append("wc differs between ranks")
    s = [mx_ref.live(p) for p in d["ws"]]
    if any((p != s[0]).any() for p in s): b.append("ws differs between ranks")
    return b
def reference(x, u, v, wc, ws):
    w = pk(wc[0], ws[0])
    lay = [pick(w, np.arange(128 * b, 128 * b + 128)) for b in range(4)]
    qu = mx_ref.quantize(u[0])
    now = [x[r] for r in range(N)]
    lists = [None] * N
    for t in range(R):
        held, score = [], []
        for r in range(N):
            q = mx_ref.quantize(now[r])
            held.append(decode(q).astype(BF))
            score.append(mx_ref.matmul(qu, q))
        for r in range(N):
            s = r ^ STEP[t]
            if s < r: continue
            e, first = segments(units(score[r], -1), units(score[s], 1))
            z = gcols(held[r], e[0]).astype(np.float32) + gcols(held[s], e[1]).astype(np.float32)
            q = mx_ref.quantize((z * np.float32(0.5)).astype(BF))
            h = tile([np.maximum(mx_ref.matmul(lay[b], q), np.float32(0.0)) * np.float32(0.03125) for b in range(4)])
            h = decode(mx_ref.quantize(h)).astype(BF)
            for i, k in ((0, r), (1, s)):
                now[k] = (held[k].astype(np.float32) + gcols(h, first[i]).astype(np.float32)).astype(BF)
                lists[k] = first[i]
    y, ol = np.zeros((N, 128, C), np.float32), np.zeros((N, 8, C), np.float32)
    oc, osc = np.zeros((N, 128, 4 * C), np.uint8), np.zeros((N, 16, C), np.uint8)
    for r in range(N):
        q = mx_ref.quantize(now[r])
        y[r] = mx_ref.matmul(mx_ref.quantize(v[r]), q)
        ol[r] = lists[r]
        oc[r], osc[r] = emit(q)
    return {"y": y, "ol": ol, "oc": oc, "osc": osc}

@@ -1,0 +1,373 @@
+from concourse.mybir import dt, AluOpType as A, ActivationFunctionType as F
+
+C = 256
+R = 3
+ND = 10
+BIG = float(2 ** 19)
+HUGE = float(2 ** 24)
+FAR = 1.0e29
+PHI = 1.25 * 2.0 ** -24
+ETA = 2.0 ** -120
+X4, U8, BF, F32, U16, I32 = "float8_e4m3fn_x4", "uint8", "bfloat16", "float32", "uint16", "int32"
+
+
+def _s(n, d):
+    return ("sbuf", [128, n], d)
+
+
+SCRATCH = {
+    "xs": _s(1024, BF), "us": _s(512, BF), "vs": _s(512, BF),
+    "q0": _s(C, X4), "p0": _s(C, U8), "uq": _s(128, X4), "up": _s(128, U8), "u1q": _s(128, X4), "u1p": _s(128, U8),
+    "u3q": _s(384, X4), "u3p": _s(384, U8),
+    "vq": _s(128, X4), "vp": _s(128, U8), "wq": _s(512, X4), "wp": _s(512, U8), "eq": _s(512, X4), "ep": _s(512, U8),
+    "nq": _s(C, X4), "np": _s(C, U8), "zq": _s(C, X4), "zp": _s(C, U8), "hq": _s(C, X4), "hp": _s(C, U8),
+    "one": _s(1024, BF), "ef": _s(528, BF),
+    "pi": _s(8, I32), "pj": _s(8, I32), "col": _s(8, F32), "row": _s(C, F32), "uli": _s(32, I32), "ul": _s(32, U16), "pl": _s(16, U16),
+    "mown": _s(C, F32), "keep": _s(C, F32), "m3": _s(C, F32), "mtmp": _s(C, F32), "mfar": _s(C, F32), "mdiag": _s(C, F32),
+    "pos": _s(C, BF), "keep3": _s(768, BF),
+    "mk": _s(C, F32), "hold": _s(C, F32), "dl": _s(C, F32), "dw": _s(16, F32), "t3": _s(C, F32), "rb": _s(288, F32),
+    "sgo": _s(768, BF), "sgp": _s(768, BF), "vv": _s(768, BF), "qo": _s(C, BF), "qp": _s(C, BF),
+    "cm": _s(272 * ND, BF), "sc": _s(136 * ND, BF), "sa": _s(272 * (16 - ND), BF),
+    "rk": _s(16, F32), "rko": _s(16, U16), "vsd": _s(C, BF), "cb": _s(C, F32),
+    "qr": _s(C, BF), "sto": _s(264, F32), "stp": _s(264, F32), "aown": _s(16, U16), "apar": _s(16, U16),
+    "wm": _s(1024, BF), "wm2": _s(1024, BF), "seg": _s(1024, BF), "fpr": _s(C, BF), "fsr": _s(C, BF), "fow": _s(C, BF), "fna": _s(C, BF),
+    "fpo": _s(16, U16), "bv": _s(C, F32), "wsg": _s(512, F32), "cum": _s(C, F32),
+    "ia": _s(16, U16), "ib": _s(16, U16), "ibi": _s(16, I32), "ibj": _s(16, I32), "fo": _s(16, U16),
+    "ola": _s(16, F32), "olb": _s(16, F32), "olc": _s(16, F32),
+    "do": _s(1024, BF), "dp": _s(1024, BF), "dos": _s(1024, BF), "dps": _s(1024, BF), "tmp": _s(1024, BF),
+    "z": _s(1024, BF), "hs": _s(272 * 4, BF), "hg": _s(1024, BF), "xn": _s(1024, BF), "ys": _s(C, F32),
+    "ps": ("psum", [128, 4096], F32),
+}
+for _t in range(R + 1):
+    SCRATCH["tc%d" % _t] = _s(C, X4)
+    SCRATCH["tp%d" % _t] = _s(C, U8)
+for _t in range(R):
+    for _n, _w, _d in (("c", C, X4), ("p", C, U8), ("l", 16, U16)):
+        SCRATCH["hop%s%d" % (_n, _t)] = _s(_w, _d)
+        SCRATCH["far%s%d" % (_n, _t)] = _s(_w, _d)
+    SCRATCH["ls%d" % _t] = _s(16, U16)
+
+SEMAPHORES = ["cv", "ca", "cp", "cg", "dx", "du", "dv", "dwc", "dws", "dout", "sent"] + \
+    ["a%s%d" % (n, t) for n in "cpl" for t in range(R)]
+
+
+def relays(T, topo, rank):
+    me = T.cores[rank]
+    far = [T.cores[rank ^ (1 << t)] for t in range(R)]
+    ok = [c for c in topo.cores_of(me) if c not in T.cores and all(topo.may_write(c, d) for d in far)]
+    ok.sort(key=lambda c: (topo.die(c) != topo.die(me), c))
+    return ok[0], ok[1]
+
+
+def view(T, name):
+    return T[name][:].bitcast(dt.uint8) if SCRATCH[name][2] == X4 else T[name][:]
+
+
+def write(g, T, topo, src, dst, out, in_, sem):
+    rid, pid = topo.addr(dst, src)
+    g.remote_dma(view(T, out), view(T, in_), T.sem[sem], T.sem.sent, pid, rid, topo.mask(src, dst))
+    return len(topo.engines(src, dst))
+
+
+def relay_program(g, core, T, topo, rank, kinds):
+    me = T.cores[rank]
+    n = 0
+    for t in range(R):
+        d = T.cores[rank ^ (1 << t)]
+        for k in kinds:
+            g.wait_ge(T.sem["a%s%d" % (k, t)], len(topo.engines(me, core)))
+            n += write(g, T, topo, core, d, "far%s%d" % (k, t), "hop%s%d" % (k, t), "a%s%d" % (k, t))
+    g.wait_ge(T.sem.sent, n)
+
+
+def rank_program(g, core, T, topo):
+    rank = T.rank_of(core)
+    if rank is None:
+        for r in range(len(T.cores)):
+            a, b = relays(T, topo, r)
+            if core == a:
+                relay_program(g, core, T, topo, r, "pl")
+            if core == b:
+                relay_program(g, core, T, topo, r, "c")
+        return
+    ra, rb_ = relays(T, topo, rank)
+    Q = {"v": g.vector, "a": g.scalar, "p": g.tensor, "g": g, "s": g.sync}
+    SEM = {"v": "cv", "a": "ca", "p": "cp", "g": "cg"}
+    count = {}
+    seen = {}
+    last_w = {}
+    readers = {}
+
+    def need(q, tok):
+        if tok is not None and seen.get((q, tok[0]), 0) < tok[1]:
+            Q[q].wait_ge(T.sem[tok[0]], tok[1])
+            seen[(q, tok[0])] = tok[1]
+
+    def order(q, rd, wr):
+        toks = {}
+        for tok in [last_w.get(k) for k in rd + wr] + [x for k in wr for x in readers.get(k, [])]:
+            if tok is not None and not (q == "p" and tok[0] == "cp"):
+                toks[tok[0]] = max(toks.get(tok[0], 0), tok[1])
+        for s in sorted(toks):
+            need(q, (s, toks[s]))
+
+    def done(ins, sem, n, rd, wr):
+        ins.then_inc(T.sem[sem], n)
+        count[sem] = count.get(sem, 0) + n
+        tok = (sem, count[sem])
+        for k in wr:
+            last_w[k] = tok
+            readers[k] = []
+        for k in rd:
+            readers.setdefault(k, []).append(tok)
+
+    def op(q, rd, wr, fn):
+        wr = wr + [k for k in rd if k[:2] == "ps"]
+        order(q, rd, wr)
+        done(fn(), SEM[q], 1, rd, wr)
+
+    def dma(q, sem, rd, wr, out, in_):
+        order(q, rd, wr)
+        done(Q[q].dma_start(out, in_), sem, 16, rd, wr)
+
+    V, S, PE = g.vector, g.scalar, g.tensor
+
+    def bank(b, n=C):
+        return T.ps[:, 512 * b:512 * b + n]
+
+    def part(name, b, n=C):
+        return T[name][:, n * b:n * b + n]
+
+    def four(name):
+        return ["%s%d" % (name, b) for b in range(4)]
+
+    def mm(b, lq, lp, a, rq, rp, start=True, stop=True):
+        op("p", [lq, rq, lp, rp], ["ps%d" % b], lambda: PE.matmul_mx(
+            bank(b), T[lq][:, a:a + 128], T[lp][:, a:a + 128], T[rq][:], T[rp][:], start, stop))
+
+    def quant(q, p, src, rd):
+        op("v", rd, [q, p], lambda: V.quantize_mx(T[q][:], T[p][:], T[src][:]))
+
+    def pick(q2, p2, q, p, key, off):
+        op("v", [q, key], [q2], lambda: V.tensor_copy(T[q2][:].bitcast(dt.uint32), T[q][:].bitcast(dt.uint32).indirect(off)))
+        op("a", [p, key], [p2], lambda: S.activation(T[p2][:], T[p][:].indirect(off), F.Copy))
+
+    def wrap(name):
+        op("v", ["mdiag", name], ["cb"], lambda: V.tensor_tensor_scan(T.cb[:], T.mdiag[:], T[name][:, 0:C], 0.0, A.add, A.max))
+
+    ends = T.cb[:, 15:C:16]
+    c0, c256, c1024, pm, pm16 = (T.col[:, j:j + 1] for j in range(5))
+
+    def unwrap(out, s1=c0, s2=None, op1=None):
+        if s2 is None:
+            op("v", ["cb", "col"], [out], lambda: V.tensor_scalar(T[out][:], ends, s1, None, A.add))
+        else:
+            op("v", ["cb", "col"], [out], lambda: V.tensor_scalar(T[out][:], ends, s1, s2, A.add, op1))
+
+    def signs(sg, m, b):
+        op("a", ["ps%d" % b], ["%s%d" % (sg, m)], lambda: S.activation(T[sg][:, m:768:3], bank(b), F.Sign, bias=-ETA))
+
+    def quantities(sg, q):
+        op("v", ["%s%d" % (sg, m) for m in range(3)] + ["keep3"], ["vv"], lambda: V.tensor_tensor_scan(T.vv[:], T.keep3[:], T[sg][:], 0.0, A.mult, A.add))
+        op("v", ["vv"], [q], lambda: V.tensor_scalar(T[q][:], T.vv[:, 2:768:3], 5.0, 0.5, A.add, A.mult))
+
+    def starts(lst, q, st, out):
+        op("v", [q, lst], ["qr"], lambda: V.tensor_copy(T.qr[:], T[q][:].indirect(T[lst][:])))
+        op("v", ["qr"], [st], lambda: V.tensor_tensor_scan(T[st][:, 1:C + 1], T.qr[:], T.qr[:], 0.0, A.add, A.max))
+        wrap(st)
+        unwrap(out)
+
+    def gather_a(out, okey, win, wkey, off):
+        op("a", [wkey, off], [okey], lambda: S.activation(out, win.indirect(T[off][:]), F.Copy))
+
+    def iota(key, pattern, base):
+        op("g", [], [key], lambda: g.iota(T[key][:], pattern, base, 0, allow_small_or_imprecise_dtypes=True))
+
+    dma("s", "dx", [], ["xs"], T.xs[:], T.x[:])
+    dma("a", "du", [], ["us"], T.us[:], T.u[:])
+    op("v", [], ["one"], lambda: V.memset(T.one[:], 1.0))
+    op("g", [], ["pi"], lambda: g.iota(T.pi[:], [[0, 8]], 0, 1))
+    iota("row", [[0, 16], [1, 16]], 0)
+    op("g", [], ["uli"], lambda: g.iota(T.uli[:], [[1, 4], [16, 8]], 0, 0))
+    op("g", ["one"], ["keep"], lambda: g.affine_select(T.keep[:], T.one[:, 0:C], [[0, 16], [1, 16]], A.is_gt, 0.0, 0, 0))
+    iota("pos", [[1, C]], 0)
+    op("v", ["pi"], ["pj"], lambda: V.tensor_scalar(T.pj[:], T.pi[:], 15, None, A.bitwise_and))
+    op("v", [], ["sto"], lambda: V.memset(T.sto[:, 0:8], 0.0))
+    op("v", ["pj"], ["pm"], lambda: V.tensor_copy(pm, T.pj[:, 0:1]))
+    op("v", [], ["stp"], lambda: V.memset(T.stp[:, 0:8], 0.0))
+    op("v", ["pm"], ["pm16"], lambda: V.tensor_scalar(pm16, pm, 16.0, None, A.mult))
+    op("v", ["pm"], ["c0"], lambda: V.tensor_scalar(c0, pm, -15.0, BIG, A.add, A.mult))
+    op("v", [], ["hsz"], lambda: V.memset(T.hs[:, C:272 * 4:272], 0.0))
+    op("v", ["c0"], ["c256"], lambda: V.tensor_scalar(c256, c0, 256.0, None, A.add))
+    op("v", ["c0", "c256"], ["col"], lambda: V.tensor_scalar(c1024, c0, -1024.0, None, A.add))
+    op("v", ["row", "pm"], ["mown"], lambda: V.tensor_scalar(T.mown[:], T.row[:], pm, None, A.is_equal))
+    op("v", ["row", "pm16"], ["pl"], lambda: V.tensor_scalar(T.pl[:], T.row[:, 0:16], pm16, None, A.add))
+    op("v", ["uli"], ["ul"], lambda: V.tensor_copy(T.ul[:], T.uli[:]))
+    op("a", ["mown"], ["mfar"], lambda: S.activation(T.mfar[:], T.mown[:], F.Copy, scale=FAR))
+    op("v", ["row", "pm"], ["mtmp"], lambda: V.tensor_scalar(T.mtmp[:], T.row[:], pm, FAR, A.is_lt, A.mult))
+    op("v", ["row", "pm"], ["cb"], lambda: V.tensor_scalar(T.cb[:], T.row[:], pm, BIG + HUGE, A.is_gt, A.mult))
+    op("a", ["cb"], ["mdiag"], lambda: S.activation(T.mdiag[:], T.cb[:], F.Identity, bias=-HUGE))
+    quant("uq", "up", "us", ["us"])
+    pick("u1q", "u1p", "uq", "up", "ul", T.ul[:, 0:8])
+    quant("q0", "p0", "xs", ["xs"])
+    pick("tc0", "tp0", "q0", "p0", "pl", T.pl[:])
+    op("v", ["mtmp", "mfar"], ["m3"], lambda: V.tensor_tensor(T.m3[:], T.mtmp[:], T.mfar[:], A.subtract))
+    sent = 0
+
+    for t in range(R):
+        buys = not rank >> t & 1
+        last = t == R - 1
+        tc, tp, ls = "tc%d" % t, "tp%d" % t, "ls%d" % t
+        fc, fp, fl = "farc%d" % t, "farp%d" % t, "farl%d" % t
+        partner = T.cores[rank ^ (1 << t)]
+        last_w[fc] = ("ac%d" % t, len(topo.engines(rb_, partner)))
+        last_w[fp] = ("ap%d" % t, len(topo.engines(ra, partner)))
+        last_w[fl] = ("al%d" % t, len(topo.engines(ra, partner)))
+        order("g", [tc], [])
+        sent += write(g, T, topo, core, rb_, "hopc%d" % t, tc, "ac%d" % t)
+        order("g", [tp], [])
+        sent += write(g, T, topo, core, ra, "hopp%d" % t, tp, "ap%d" % t)
+        if t == 0:
+            op("g", ["one"], ["ef"], lambda: g.affine_select(T.ef[:], T.one[:, 0:528], [[-1, 528]], A.is_equal, 0.0, 3, 4))
+            op("g", ["one"], ["keep3"], lambda: g.affine_select(T.keep3[:], T.one[:, 0:768], [[0, C], [1, 3]], A.is_gt, 0.0, 0, 0))
+        else:
+            iota("wsg", [[0, 512]], 1)
+        iota("wm", [[0, 1024]], 0)
+        mm(0, "u1q", "u1p", 0, tc, tp)
+        mm(1, "u1q", "u1p", 0, tc, tp)
+        way = A.add if buys else A.subtract
+        own = T.hold[:, 15:C:16]
+        op("v", ["ps0", "mown"], ["mk"], lambda: V.tensor_tensor(T.mk[:], bank(0), T.mown[:], A.mult))
+        op("a", ["ps1"], ["dl"], lambda: S.activation(T.dl[:], bank(1), F.Abs, bias=ETA, scale=PHI if buys else -PHI))
+        if t == 0:
+            dma("s", "dwc", ["dl"], ["wq"], view(T, "wq"), T.wc[:])
+            dma("s", "dws", [], ["wp"], T.wp[:], T.ws[:])
+            dma("s", "dv", [], ["vs"], T.vs[:], T.v[:])
+        else:
+            for m in range(3):
+                mm(2 + m, "u3q", "u3p", 128 * m, tc, tp)
+            signs("sgo", 0, 2)
+        op("v", ["mk", "keep"], ["hold"], lambda: V.tensor_tensor_scan(T.hold[:], T.keep[:], T.mk[:], 0.0, A.mult, way))
+        op("v", ["dl", "m3"], ["t3"], lambda: V.tensor_tensor(T.t3[:], T.dl[:], T.m3[:], A.min))
+        op("a", ["hold"], ["dw"], lambda: S.activation(T.dw[:], own, F.Abs, bias=ETA, scale=PHI))
+        op("a", ["hold"], ["rb0"], lambda: S.activation(T.rb[:, 0:16], own, F.Copy))
+        op("v", ["t3", "ps0"], ["rb1"], lambda: V.tensor_tensor(T.rb[:, 16:272], T.t3[:], bank(0), way))
+        op("v", ["hold", "dw"], ["rb2"], lambda: V.tensor_tensor(T.rb[:, 272:288], own, T.dw[:], A.add))
+        if t > 0:
+            signs("sgo", 1, 3)
+            signs("sgo", 2, 4)
+        rbs = ["rb0", "rb1", "rb2"]
+        for k in range(ND):
+            op("v", rbs, ["cm%d" % k], lambda: V.tensor_scalar(part("cm", k, 272), T.rb[:, k:k + 272], T.rb[:, k:k + 1], None, A.is_gt))
+        for k in range(ND, 16):
+            op("a", rbs, ["sa%d" % k], lambda: S.activation(
+                part("sa", k - ND, 272), T.rb[:, k:k + 272], F.Sign, bias=T.rb[:, k:k + 1], scale=-1.0))
+        for k in range(ND, 16):
+            op("a", ["sa%d" % k], ["sa%d" % k, "rk%d" % k], lambda: S.activation(
+                part("sa", k - ND, 272), part("sa", k - ND, 272), F.Relu, scale=-1.0, accum_out=T.rk[:, k:k + 1]))
+        for k in range(ND):
+            op("v", ["cm%d" % k], ["sc%d" % k], lambda: V.tensor_tensor_scan(
+                part("sc", k, 136), part("cm", 2 * k, 136), part("cm", 2 * k + 1, 136), 0.0, A.add, A.add))
+        op("v", ["sc%d" % k for k in range(ND)], ["rkv"], lambda: V.tensor_scalar(T.rko[:, 0:ND], T.sc[:, 135:136 * ND:136], 0.0, None, A.add))
+        op("v", ["rk%d" % k for k in range(ND, 16)], ["rko"], lambda: V.tensor_copy(T.rko[:, ND:16], T.rk[:, ND:16]))
+        op("v", ["pos", "rkv", "rko"], ["vsd"], lambda: V.tensor_copy(T.vsd[:].indirect(T.rko[:]), T.pos[:]))
+        wrap("vsd")
+        unwrap(ls)
+        order("g", [ls], [])
+        sent += write(g, T, topo, core, ra, "hopl%d" % t, ls, "al%d" % t)
+        if t == 0:
+            iota("wsg", [[0, 512]], 1)
+            pick("u3q", "u3p", "uq", "up", "ul", T.ul[:, 8:32])
+            for b in range(4):
+                op("v", ["ef"], ["eq", "ep"] if b == 3 else ["eq%d" % b], lambda: V.quantize_mx(
+                    part("eq", b, 128), part("ep", b, 128), T.ef[:, 3 - b:515 - b]))
+            for m in range(3):
+                mm(2 + m, "u3q", "u3p", 128 * m, tc, tp)
+                signs("sgo", m, 2 + m)
+        for b in range(4):
+            mm(b, "eq", "ep", 128 * b, tc, tp)
+        for m in range(3):
+            mm(5 + m, "u3q", "u3p", 128 * m, fc, fp)
+            signs("sgp", m, 5 + m)
+        for b in range(4):
+            op("a", ["ps%d" % b], ["do%d" % b], lambda: S.activation(part("do", b), bank(b), F.Copy, scale=0.5))
+        for b in range(4):
+            mm(4 + b, "eq", "ep", 128 * b, fc, fp)
+        quantities("sgo", "qo")
+        starts(ls, "qo", "sto", "aown")
+        op("v", ["one", "aown"], ["wm"], lambda: V.tensor_copy(T.wm[:].indirect(T.aown[:]), T.one[:, 0:C]))
+        op("g", ["wm"], ["wm2"], lambda: g.affine_select(T.wm2[:], T.wm[:], [[0, 1024]], A.is_gt, 0.0, 1, 0))
+        quantities("sgp", "qp")
+        if last:
+            pick("nq", "np", tc, tp, "pl", T.pl[:])
+        for b in range(4):
+            mm(b, "eq", "ep", 128 * b, "nq" if last else tc, "np" if last else tp, True, False)
+        for b in range(4):
+            op("a", ["ps%d" % (4 + b)], ["dp%d" % b], lambda: S.activation(part("dp", b), bank(4 + b), F.Copy, scale=0.5))
+        for b in range(4):
+            gather_a(part("dos", b), "dos%d" % b, part("do", b), "do%d" % b, ls)
+        if t == 1:
+            quant("vq", "vp", "vs", ["vs"])
+        starts(fl, "qp", "stp", "apar")
+        for b in range(2):
+            gather_a(part("dps", b), "dps%d" % b, part("dp", b), "dp%d" % b, fl)
+        op("a", ["wm2", "apar"], ["bv"], lambda: S.activation(T.bv[:], T.wm2[:].indirect(T.apar[:]), F.Identity, bias=1024.0))
+        for b in range(2, 4):
+            gather_a(part("dps", b), "dps%d" % b, part("dp", b), "dp%d" % b, fl)
+        op("v", ["one", "apar"], ["wm"], lambda: V.tensor_copy(T.wm[:].indirect(T.apar[:]), T.one[:, 0:C]))
+        op("v", ["wm", "one"], ["seg"], lambda: V.tensor_tensor_scan(T.seg[:], T.one[:], T.wm[:], -257.0, A.mult, A.add))
+        op("v", ["seg", "apar"], ["fpr"], lambda: V.tensor_copy(T.fpr[:], T.seg[:].indirect(T.apar[:])))
+        gather_a(T.fsr[:], "fsr", T.seg[:], "seg", "aown")
+        op("a", ["fsr", "rko", "rkv"], ["fow"], lambda: S.activation(T.fow[:], T.fsr[:].indirect(T.rko[:]), F.Copy))
+        if last:
+            gather_a(T.fna[:], "fna", T.fow[:], "fow", "pl")
+        wrap("fpr")
+        unwrap("fpo", c256)
+        op("v", ["bv", "fpo"], ["wsg"], lambda: V.tensor_copy(T.wsg[:].indirect(T.fpo[:]), T.bv[:]))
+        op("v", ["wsg"], ["cum"], lambda: V.tensor_tensor_scan(T.cum[:], T.wsg[:, 0:C], T.wsg[:, 0:C], 0.0, A.add, A.max))
+        wrap("cum")
+        unwrap("ia", c1024, 1.0 / 1024, A.mult)
+        unwrap("ibi", c0, -1.0, A.add)
+        op("v", ["ibi"], ["ibj"], lambda: V.tensor_scalar(T.ibj[:], T.ibi[:], 1023, None, A.bitwise_and))
+        op("v", ["ibj"], ["ib"], lambda: V.tensor_copy(T.ib[:], T.ibj[:]))
+        for b in range(4):
+            gather_a(part("tmp", b), "tmp%d" % b, part("dps", b), "dps%d" % b, "ia")
+            op("v", ["dos%d" % b, "ib", "tmp%d" % b], ["z%d" % b], lambda: V.tensor_tensor(
+                T.z[:, b:1024:4], part("dos", b).indirect(T.ib[:]), part("tmp", b), A.add))
+        quant("zq", "zp", "z", four("z"))
+        for b in range(4):
+            mm(4 + b, "wq", "wp", 128 * b, "zq", "zp")
+        wrap("fna" if last else "fow")
+        unwrap("fo", c256, 256.0, A.min)
+        for b in (0, 2):
+            op("a", ["ps%d" % (4 + b), "hsz"], ["hs%d" % b], lambda: S.activation(T.hs[:, 272 * b:272 * b + C], bank(4 + b), F.Relu, scale=0.03125))
+        for b in (1, 3):
+            op("v", ["ps%d" % (4 + b), "hsz"], ["hs%d" % b], lambda: V.tensor_scalar(T.hs[:, 272 * b:272 * b + C], bank(4 + b), 0.0, 0.03125, A.max, A.mult))
+        for b in (0, 2):
+            gather_a(T.hg[:, b:1024:4], "hg%d" % b, T.hs[:, 272 * b:272 * b + C + 1], "hs%d" % b, "fo")
+        for b in (1, 3):
+            op("v", ["hs%d" % b, "fo"], ["hg%d" % b], lambda: V.tensor_copy(T.hg[:, b:1024:4], T.hs[:, 272 * b:272 * b + C + 1].indirect(T.fo[:])))
+        quant("hq", "hp", "hg", four("hg"))
+        for b in range(4):
+            mm(b, "eq", "ep", 128 * b, "hq", "hp", False, True)
+        if last:
+            wrap("fow")
+        for b in (0, 2):
+            op("a", ["ps%d" % b], ["xn%d" % b], lambda: S.activation(T.xn[:, b:1024:4], bank(b), F.Copy))
+            op("v", ["ps%d" % (b + 1)], ["xn%d" % (b + 1)], lambda: V.tensor_copy(T.xn[:, b + 1:1024:4], bank(b + 1)))
+        quant("tc%d" % (t + 1), "tp%d" % (t + 1), "xn", four("xn"))
+
+    tc, tp = "tc%d" % R, "tp%d" % R
+    mm(4, "vq", "vp", 0, tc, tp)
+    dma("s", "dout", [tc], [], T.oc[:], view(T, tc))
+    unwrap("ola", c256, 256.0, A.min)
+    op("v", ["ola"], ["olb"], lambda: V.tensor_scalar(T.olb[:], T.ola[:], 256.0, -257.0, A.is_ge, A.mult))
+    op("v", ["ps4"], ["ys"], lambda: V.tensor_copy(T.ys[:], bank(4)))
+    op("v", ["ola", "olb"], ["olc"], lambda: V.tensor_tensor(T.olc[:], T.ola[:], T.olb[:], A.add))
+    for k in range(4):
+        dma("a", "dout", [tp], [], T.osc[4 * k:4 * k + 4, :], T[tp][32 * k:32 * k + 4, :])
+    dma("s", "dout", ["ys"], [], T.y[:], T.ys[:])
+    dma("s", "dout", ["olc"], [], T.ol[:], T.olc[:])
+    g.wait_ge(T.sem.sent, sent)
+    for s in sorted(count):
+        need("g", (s, count[s]))

@@ -2,10 +2,11 @@ from concourse.mybir import dt, AluOpType as A, ActivationFunctionType as F
 
 C = 256
 R = 3
-ND = 10
+ND = 9
 BIG = float(2 ** 19)
 HUGE = float(2 ** 24)
-FAR = 1.0e29
+FAR = 2.0 ** 92
+LOW = 4096.0
 PHI = 1.25 * 2.0 ** -24
 ETA = 2.0 ** -120
 X4, U8, BF, F32, U16, I32 = "float8_e4m3fn_x4", "uint8", "bfloat16", "float32", "uint16", "int32"
@@ -22,18 +23,18 @@ SCRATCH = {
     "vq": _s(128, X4), "vp": _s(128, U8), "wq": _s(512, X4), "wp": _s(512, U8), "eq": _s(512, X4), "ep": _s(512, U8),
     "nq": _s(C, X4), "np": _s(C, U8), "zq": _s(C, X4), "zp": _s(C, U8), "hq": _s(C, X4), "hp": _s(C, U8),
     "one": _s(1024, BF), "ef": _s(528, BF),
-    "pi": _s(8, I32), "pj": _s(8, I32), "col": _s(8, F32), "row": _s(C, F32), "uli": _s(32, I32), "ul": _s(32, U16), "pl": _s(16, U16),
-    "mown": _s(C, F32), "keep": _s(C, F32), "m3": _s(C, F32), "mtmp": _s(C, F32), "mfar": _s(C, F32), "mdiag": _s(C, F32),
-    "pos": _s(C, BF), "keep3": _s(768, BF),
-    "mk": _s(C, F32), "hold": _s(C, F32), "dl": _s(C, F32), "dw": _s(16, F32), "t3": _s(C, F32), "rb": _s(288, F32),
-    "sgo": _s(768, BF), "sgp": _s(768, BF), "vv": _s(768, BF), "qo": _s(C, BF), "qp": _s(C, BF),
+    "pi": _s(8, I32), "pj": _s(8, I32), "col": _s(16, F32), "row": _s(C, BF), "uli": _s(32, I32), "ul": _s(32, U16), "pl": _s(16, U16),
+    "mown": _s(C, BF), "keep": _s(C, BF), "m3": _s(C, BF), "m2": _s(C, BF), "mtmp": _s(C, BF), "mfar": _s(272, BF), "msg": _s(C, BF), "mdiag": _s(C, F32),
+    "pos": _s(C, F32), "keep3": _s(768, BF), "qt": _s(1024, BF), "ft": _s(272, F32),
+    "mk": _s(C, F32), "hold": _s(C, F32), "dl": _s(C, BF), "dw": _s(16, F32), "t3": _s(C, BF), "rb": _s(288, F32),
+    "sgo": _s(768, BF), "vv": _s(768, BF), "pay": _s(C, F32),
     "cm": _s(272 * ND, BF), "sc": _s(136 * ND, BF), "sa": _s(272 * (16 - ND), BF),
-    "rk": _s(16, F32), "rko": _s(16, U16), "vsd": _s(C, BF), "cb": _s(C, F32),
+    "rk": _s(16, F32), "rko": _s(16, U16), "vsd": _s(C, F32), "cb": _s(C, F32), "cbh": _s(C, BF),
+    "lo": _s(16, U16), "lp": _s(16, U16),
     "qr": _s(C, BF), "sto": _s(264, F32), "stp": _s(264, F32), "aown": _s(16, U16), "apar": _s(16, U16),
     "wm": _s(1024, BF), "wm2": _s(1024, BF), "seg": _s(1024, BF), "fpr": _s(C, BF), "fsr": _s(C, BF), "fow": _s(C, BF), "fna": _s(C, BF),
     "fpo": _s(16, U16), "bv": _s(C, F32), "wsg": _s(512, F32), "cum": _s(C, F32),
-    "ia": _s(16, U16), "ib": _s(16, U16), "ibi": _s(16, I32), "ibj": _s(16, I32), "fo": _s(16, U16),
-    "ola": _s(16, F32), "olb": _s(16, F32), "olc": _s(16, F32),
+    "ia": _s(16, U16), "ib": _s(16, U16), "ibi": _s(16, I32), "ibj": _s(16, I32), "fo": _s(16, U16), "olr": _s(C, F32),
     "do": _s(1024, BF), "dp": _s(1024, BF), "dos": _s(1024, BF), "dps": _s(1024, BF), "tmp": _s(1024, BF),
     "z": _s(1024, BF), "hs": _s(272 * 4, BF), "hg": _s(1024, BF), "xn": _s(1024, BF), "ys": _s(C, F32),
     "ps": ("psum", [128, 4096], F32),
@@ -156,62 +157,62 @@ def rank_program(g, core, T, topo):
         op("v", ["mdiag", name], ["cb"], lambda: V.tensor_tensor_scan(T.cb[:], T.mdiag[:], T[name][:, 0:C], 0.0, A.add, A.max))
 
     ends = T.cb[:, 15:C:16]
-    c0, c256, c1024, pm, pm16 = (T.col[:, j:j + 1] for j in range(5))
+    c0, c256, c1024, clist, cplace, pm, pm16, pmh = (T.col[:, j:j + 1] for j in range(8))
 
-    def unwrap(out, s1=c0, s2=None, op1=None):
+    def unwrap(out, key, s1, s2=None, op1=None):
         if s2 is None:
-            op("v", ["cb", "col"], [out], lambda: V.tensor_scalar(T[out][:], ends, s1, None, A.add))
+            op("v", ["cb", key], [out], lambda: V.tensor_scalar(T[out][:], ends, s1, None, A.add))
         else:
-            op("v", ["cb", "col"], [out], lambda: V.tensor_scalar(T[out][:], ends, s1, s2, A.add, op1))
+            op("v", ["cb", key], [out], lambda: V.tensor_scalar(T[out][:], ends, s1, s2, A.add, op1))
 
-    def signs(sg, m, b):
-        op("a", ["ps%d" % b], ["%s%d" % (sg, m)], lambda: S.activation(T[sg][:, m:768:3], bank(b), F.Sign, bias=-ETA))
+    def signs(m):
+        op("a", ["ps%d" % (2 + m)], ["sgo%d" % m], lambda: S.activation(T.sgo[:, m:768:3], bank(2 + m), F.Sign, bias=-ETA))
 
-    def quantities(sg, q):
-        op("v", ["%s%d" % (sg, m) for m in range(3)] + ["keep3"], ["vv"], lambda: V.tensor_tensor_scan(T.vv[:], T.keep3[:], T[sg][:], 0.0, A.mult, A.add))
-        op("v", ["vv"], [q], lambda: V.tensor_scalar(T[q][:], T.vv[:, 2:768:3], 5.0, 0.5, A.add, A.mult))
-
-    def starts(lst, q, st, out):
-        op("v", [q, lst], ["qr"], lambda: V.tensor_copy(T.qr[:], T[q][:].indirect(T[lst][:])))
+    def starts(lst, st, out, between):
+        op("v", ["qt", lst], ["qr"], lambda: V.tensor_copy(T.qr[:], T.qt[:].indirect(T[lst][:])))
+        between()
         op("v", ["qr"], [st], lambda: V.tensor_tensor_scan(T[st][:, 1:C + 1], T.qr[:], T.qr[:], 0.0, A.add, A.max))
         wrap(st)
-        unwrap(out)
+        unwrap(out, "c0", c0)
 
     def gather_a(out, okey, win, wkey, off):
         op("a", [wkey, off], [okey], lambda: S.activation(out, win.indirect(T[off][:]), F.Copy))
 
-    def iota(key, pattern, base):
-        op("g", [], [key], lambda: g.iota(T[key][:], pattern, base, 0, allow_small_or_imprecise_dtypes=True))
+    def iota(key, pattern, base, out=None):
+        op("g", [], [key], lambda: g.iota(T[key][:] if out is None else out, pattern, base, 0, allow_small_or_imprecise_dtypes=True))
+
+    def column(key, out, add):
+        op("a", ["c0"], [key], lambda: S.activation(out, c0, F.Identity, bias=add))
 
     dma("s", "dx", [], ["xs"], T.xs[:], T.x[:])
     dma("a", "du", [], ["us"], T.us[:], T.u[:])
     op("v", [], ["one"], lambda: V.memset(T.one[:], 1.0))
     op("g", [], ["pi"], lambda: g.iota(T.pi[:], [[0, 8]], 0, 1))
-    iota("row", [[0, 16], [1, 16]], 0)
     op("g", [], ["uli"], lambda: g.iota(T.uli[:], [[1, 4], [16, 8]], 0, 0))
-    op("g", ["one"], ["keep"], lambda: g.affine_select(T.keep[:], T.one[:, 0:C], [[0, 16], [1, 16]], A.is_gt, 0.0, 0, 0))
-    iota("pos", [[1, C]], 0)
+    iota("row", [[0, 16], [1, 16]], 0)
+    op("g", ["one"], ["ef"], lambda: g.affine_select(T.ef[:], T.one[:, 0:528], [[-1, 528]], A.is_equal, 0.0, 3, 4))
+    iota("pos", [[8, C]], 3 - int(LOW))
     op("v", ["pi"], ["pj"], lambda: V.tensor_scalar(T.pj[:], T.pi[:], 15, None, A.bitwise_and))
-    op("v", [], ["sto"], lambda: V.memset(T.sto[:, 0:8], 0.0))
-    op("v", ["pj"], ["pm"], lambda: V.tensor_copy(pm, T.pj[:, 0:1]))
-    op("v", [], ["stp"], lambda: V.memset(T.stp[:, 0:8], 0.0))
-    op("v", ["pm"], ["pm16"], lambda: V.tensor_scalar(pm16, pm, 16.0, None, A.mult))
-    op("v", ["pm"], ["c0"], lambda: V.tensor_scalar(c0, pm, -15.0, BIG, A.add, A.mult))
-    op("v", [], ["hsz"], lambda: V.memset(T.hs[:, C:272 * 4:272], 0.0))
-    op("v", ["c0"], ["c256"], lambda: V.tensor_scalar(c256, c0, 256.0, None, A.add))
-    op("v", ["c0", "c256"], ["col"], lambda: V.tensor_scalar(c1024, c0, -1024.0, None, A.add))
-    op("v", ["row", "pm"], ["mown"], lambda: V.tensor_scalar(T.mown[:], T.row[:], pm, None, A.is_equal))
-    op("v", ["row", "pm16"], ["pl"], lambda: V.tensor_scalar(T.pl[:], T.row[:, 0:16], pm16, None, A.add))
     op("v", ["uli"], ["ul"], lambda: V.tensor_copy(T.ul[:], T.uli[:]))
-    op("a", ["mown"], ["mfar"], lambda: S.activation(T.mfar[:], T.mown[:], F.Copy, scale=FAR))
-    op("v", ["row", "pm"], ["mtmp"], lambda: V.tensor_scalar(T.mtmp[:], T.row[:], pm, FAR, A.is_lt, A.mult))
-    op("v", ["row", "pm"], ["cb"], lambda: V.tensor_scalar(T.cb[:], T.row[:], pm, BIG + HUGE, A.is_gt, A.mult))
-    op("a", ["cb"], ["mdiag"], lambda: S.activation(T.mdiag[:], T.cb[:], F.Identity, bias=-HUGE))
+    op("v", ["pj"], ["pm"], lambda: V.tensor_copy(pm, T.pj[:, 0:1]))
+    op("v", [], ["mfz"], lambda: V.memset(T.mfar[:, 0:16], 0.0))
+    op("a", ["pm"], ["pmh"], lambda: S.activation(pmh, pm, F.Identity, bias=-0.5, scale=-1.0))
+    op("a", ["pm"], ["pm16"], lambda: S.activation(pm16, pm, F.Copy, scale=16.0))
+    op("a", ["pm"], ["c0"], lambda: S.activation(c0, pm, F.Identity, bias=-15.0 * BIG, scale=BIG))
+    op("v", ["row", "pm"], ["mown"], lambda: V.tensor_scalar(T.mown[:], T.row[:], pm, None, A.is_equal))
+    op("v", ["row", "pm"], ["mtmp"], lambda: V.tensor_scalar(T.mtmp[:], T.row[:], pm, 4 * FAR, A.is_lt, A.mult))
+    op("v", ["row"], ["keep"], lambda: V.tensor_scalar(T.keep[:], T.row[:], 0.0, None, A.is_gt))
+    op("v", ["row", "pm16"], ["pl"], lambda: V.tensor_scalar(T.pl[:], T.row[:, 0:16], pm16, None, A.add))
+    op("a", ["mown"], ["mfar"], lambda: S.activation(T.mfar[:, 16:272], T.mown[:], F.Copy, scale=FAR))
+    op("a", ["row", "pmh"], ["msg"], lambda: S.activation(T.msg[:], T.row[:], F.Sign, bias=pmh))
+    op("a", ["msg"], ["mdiag"], lambda: S.activation(T.mdiag[:], T.msg[:], F.Identity, bias=(BIG - HUGE) / 2, scale=(BIG + HUGE) / 2))
+    op("v", ["mfar", "mfz"], ["m2"], lambda: V.tensor_tensor(T.m2[:], T.mfar[:, 15:271], T.mfar[:, 16:272], A.subtract))
+    op("v", ["m2", "mtmp"], ["m3"], lambda: V.tensor_tensor(T.m3[:], T.mtmp[:], T.m2[:], A.add))
     quant("uq", "up", "us", ["us"])
     pick("u1q", "u1p", "uq", "up", "ul", T.ul[:, 0:8])
     quant("q0", "p0", "xs", ["xs"])
     pick("tc0", "tp0", "q0", "p0", "pl", T.pl[:])
-    op("v", ["mtmp", "mfar"], ["m3"], lambda: V.tensor_tensor(T.m3[:], T.mtmp[:], T.mfar[:], A.subtract))
+    pick("u3q", "u3p", "uq", "up", "ul", T.ul[:, 8:32])
     sent = 0
 
     for t in range(R):
@@ -228,13 +229,16 @@ def rank_program(g, core, T, topo):
         order("g", [tp], [])
         sent += write(g, T, topo, core, ra, "hopp%d" % t, tp, "ap%d" % t)
         if t == 0:
-            op("g", ["one"], ["ef"], lambda: g.affine_select(T.ef[:], T.one[:, 0:528], [[-1, 528]], A.is_equal, 0.0, 3, 4))
             op("g", ["one"], ["keep3"], lambda: g.affine_select(T.keep3[:], T.one[:, 0:768], [[0, C], [1, 3]], A.is_gt, 0.0, 0, 0))
+            iota("qt", [[0, C], [1, 4]], 1)
+            iota("sto", [[0, 8]], 0, T.sto[:, 0:8])
         else:
             iota("wsg", [[0, 512]], 1)
         iota("wm", [[0, 1024]], 0)
         mm(0, "u1q", "u1p", 0, tc, tp)
         mm(1, "u1q", "u1p", 0, tc, tp)
+        for m in range(3):
+            mm(2 + m, "u3q", "u3p", 128 * m, tc, tp)
         way = A.add if buys else A.subtract
         own = T.hold[:, 15:C:16]
         op("v", ["ps0", "mown"], ["mk"], lambda: V.tensor_tensor(T.mk[:], bank(0), T.mown[:], A.mult))
@@ -243,19 +247,15 @@ def rank_program(g, core, T, topo):
             dma("s", "dwc", ["dl"], ["wq"], view(T, "wq"), T.wc[:])
             dma("s", "dws", [], ["wp"], T.wp[:], T.ws[:])
             dma("s", "dv", [], ["vs"], T.vs[:], T.v[:])
-        else:
-            for m in range(3):
-                mm(2 + m, "u3q", "u3p", 128 * m, tc, tp)
-            signs("sgo", 0, 2)
+        signs(0)
         op("v", ["mk", "keep"], ["hold"], lambda: V.tensor_tensor_scan(T.hold[:], T.keep[:], T.mk[:], 0.0, A.mult, way))
-        op("v", ["dl", "m3"], ["t3"], lambda: V.tensor_tensor(T.t3[:], T.dl[:], T.m3[:], A.min))
+        op("v", ["dl", "m3"], ["t3"], lambda: V.tensor_tensor_scan(T.t3[:], T.m3[:], T.dl[:], 0.0, A.add, A.min))
         op("a", ["hold"], ["dw"], lambda: S.activation(T.dw[:], own, F.Abs, bias=ETA, scale=PHI))
         op("a", ["hold"], ["rb0"], lambda: S.activation(T.rb[:, 0:16], own, F.Copy))
         op("v", ["t3", "ps0"], ["rb1"], lambda: V.tensor_tensor(T.rb[:, 16:272], T.t3[:], bank(0), way))
         op("v", ["hold", "dw"], ["rb2"], lambda: V.tensor_tensor(T.rb[:, 272:288], own, T.dw[:], A.add))
-        if t > 0:
-            signs("sgo", 1, 3)
-            signs("sgo", 2, 4)
+        signs(1)
+        signs(2)
         rbs = ["rb0", "rb1", "rb2"]
         for k in range(ND):
             op("v", rbs, ["cm%d" % k], lambda: V.tensor_scalar(part("cm", k, 272), T.rb[:, k:k + 272], T.rb[:, k:k + 1], None, A.is_gt))
@@ -265,69 +265,73 @@ def rank_program(g, core, T, topo):
         for k in range(ND, 16):
             op("a", ["sa%d" % k], ["sa%d" % k, "rk%d" % k], lambda: S.activation(
                 part("sa", k - ND, 272), part("sa", k - ND, 272), F.Relu, scale=-1.0, accum_out=T.rk[:, k:k + 1]))
+        op("v", ["sgo0", "sgo1", "sgo2", "keep3"], ["vv"], lambda: V.tensor_tensor_scan(T.vv[:], T.keep3[:], T.sgo[:], 0.0, A.mult, A.add))
         for k in range(ND):
             op("v", ["cm%d" % k], ["sc%d" % k], lambda: V.tensor_tensor_scan(
                 part("sc", k, 136), part("cm", 2 * k, 136), part("cm", 2 * k + 1, 136), 0.0, A.add, A.add))
+        op("v", ["vv", "pos"], ["pay"], lambda: V.tensor_tensor_scan(T.pay[:], T.vv[:, 2:768:3], T.pos[:], -LOW, A.max, A.add))
+        if t == 0:
+            column("clist", clist, LOW)
+            column("cplace", cplace, LOW - 3.0)
+            column("c256", c256, 256.0)
+            column("c1024", c1024, -1024.0)
         op("v", ["sc%d" % k for k in range(ND)], ["rkv"], lambda: V.tensor_scalar(T.rko[:, 0:ND], T.sc[:, 135:136 * ND:136], 0.0, None, A.add))
         op("v", ["rk%d" % k for k in range(ND, 16)], ["rko"], lambda: V.tensor_copy(T.rko[:, ND:16], T.rk[:, ND:16]))
-        op("v", ["pos", "rkv", "rko"], ["vsd"], lambda: V.tensor_copy(T.vsd[:].indirect(T.rko[:]), T.pos[:]))
+        op("v", ["pay", "rkv", "rko"], ["vsd"], lambda: V.tensor_copy(T.vsd[:].indirect(T.rko[:]), T.pay[:]))
         wrap("vsd")
-        unwrap(ls)
+        unwrap(ls, "clist", clist, 0.5, A.mult)
         order("g", [ls], [])
         sent += write(g, T, topo, core, ra, "hopl%d" % t, ls, "al%d" % t)
         if t == 0:
+            iota("stp", [[0, 8]], 0, T.stp[:, 0:8])
             iota("wsg", [[0, 512]], 1)
-            pick("u3q", "u3p", "uq", "up", "ul", T.ul[:, 8:32])
             for b in range(4):
                 op("v", ["ef"], ["eq", "ep"] if b == 3 else ["eq%d" % b], lambda: V.quantize_mx(
                     part("eq", b, 128), part("ep", b, 128), T.ef[:, 3 - b:515 - b]))
-            for m in range(3):
-                mm(2 + m, "u3q", "u3p", 128 * m, tc, tp)
-                signs("sgo", m, 2 + m)
         for b in range(4):
             mm(b, "eq", "ep", 128 * b, tc, tp)
-        for m in range(3):
-            mm(5 + m, "u3q", "u3p", 128 * m, fc, fp)
-            signs("sgp", m, 5 + m)
-        for b in range(4):
-            op("a", ["ps%d" % b], ["do%d" % b], lambda: S.activation(part("do", b), bank(b), F.Copy, scale=0.5))
         for b in range(4):
             mm(4 + b, "eq", "ep", 128 * b, fc, fp)
-        quantities("sgo", "qo")
-        starts(ls, "qo", "sto", "aown")
+        for b in range(4):
+            op("a", ["ps%d" % b], ["do%d" % b], lambda: S.activation(part("do", b), bank(b), F.Copy, scale=0.5))
+        unwrap("lo", "cplace", cplace, 0.125, A.mult)
+        starts(ls, "sto", "aown", lambda: None)
         op("v", ["one", "aown"], ["wm"], lambda: V.tensor_copy(T.wm[:].indirect(T.aown[:]), T.one[:, 0:C]))
         op("g", ["wm"], ["wm2"], lambda: g.affine_select(T.wm2[:], T.wm[:], [[0, 1024]], A.is_gt, 0.0, 1, 0))
-        quantities("sgp", "qp")
+        if t == 0:
+            iota("hsz", [[0, 4]], 0, T.hs[:, C:272 * 4:272])
+        if t == 1:
+            iota("ft", [[1, 272]], 0)
+            iota("ft", [[0, 8]], -1, T.ft[:, C:C + 8])
+            quant("vq", "vp", "vs", ["vs"])
+        for b in range(4):
+            op("a", ["ps%d" % (4 + b)], ["dp%d" % b], lambda: S.activation(part("dp", b), bank(4 + b), F.Copy, scale=0.5))
         if last:
             pick("nq", "np", tc, tp, "pl", T.pl[:])
         for b in range(4):
             mm(b, "eq", "ep", 128 * b, "nq" if last else tc, "np" if last else tp, True, False)
         for b in range(4):
-            op("a", ["ps%d" % (4 + b)], ["dp%d" % b], lambda: S.activation(part("dp", b), bank(4 + b), F.Copy, scale=0.5))
-        for b in range(4):
-            gather_a(part("dos", b), "dos%d" % b, part("do", b), "do%d" % b, ls)
-        if t == 1:
-            quant("vq", "vp", "vs", ["vs"])
-        starts(fl, "qp", "stp", "apar")
+            gather_a(part("dos", b), "dos%d" % b, part("do", b), "do%d" % b, "lo")
+        starts(fl, "stp", "apar", lambda: op("v", [fl], ["lp"], lambda: V.tensor_scalar(T.lp[:], T[fl][:], 0.25, -0.375, A.mult, A.add)))
         for b in range(2):
-            gather_a(part("dps", b), "dps%d" % b, part("dp", b), "dp%d" % b, fl)
+            gather_a(part("dps", b), "dps%d" % b, part("dp", b), "dp%d" % b, "lp")
         op("a", ["wm2", "apar"], ["bv"], lambda: S.activation(T.bv[:], T.wm2[:].indirect(T.apar[:]), F.Identity, bias=1024.0))
         for b in range(2, 4):
-            gather_a(part("dps", b), "dps%d" % b, part("dp", b), "dp%d" % b, fl)
+            gather_a(part("dps", b), "dps%d" % b, part("dp", b), "dp%d" % b, "lp")
         op("v", ["one", "apar"], ["wm"], lambda: V.tensor_copy(T.wm[:].indirect(T.apar[:]), T.one[:, 0:C]))
         op("v", ["wm", "one"], ["seg"], lambda: V.tensor_tensor_scan(T.seg[:], T.one[:], T.wm[:], -257.0, A.mult, A.add))
-        op("v", ["seg", "apar"], ["fpr"], lambda: V.tensor_copy(T.fpr[:], T.seg[:].indirect(T.apar[:])))
+        op("v", ["seg", "apar", "mown"], ["fpr"], lambda: V.tensor_tensor(T.fpr[:], T.seg[:].indirect(T.apar[:]), T.mown[:], A.mult))
         gather_a(T.fsr[:], "fsr", T.seg[:], "seg", "aown")
         op("a", ["fsr", "rko", "rkv"], ["fow"], lambda: S.activation(T.fow[:], T.fsr[:].indirect(T.rko[:]), F.Copy))
         if last:
             gather_a(T.fna[:], "fna", T.fow[:], "fow", "pl")
-        wrap("fpr")
-        unwrap("fpo", c256)
+        op("v", ["fpr", "keep"], ["cbh"], lambda: V.tensor_tensor_scan(T.cbh[:], T.keep[:], T.fpr[:], 0.0, A.mult, A.add))
+        op("v", ["cbh"], ["fpo"], lambda: V.tensor_scalar(T.fpo[:], T.cbh[:, 15:C:16], 256.0, None, A.add))
         op("v", ["bv", "fpo"], ["wsg"], lambda: V.tensor_copy(T.wsg[:].indirect(T.fpo[:]), T.bv[:]))
         op("v", ["wsg"], ["cum"], lambda: V.tensor_tensor_scan(T.cum[:], T.wsg[:, 0:C], T.wsg[:, 0:C], 0.0, A.add, A.max))
         wrap("cum")
-        unwrap("ia", c1024, 1.0 / 1024, A.mult)
-        unwrap("ibi", c0, -1.0, A.add)
+        unwrap("ia", "c1024", c1024, 1.0 / 1024, A.mult)
+        unwrap("ibi", "c0", c0, -1.0, A.add)
         op("v", ["ibi"], ["ibj"], lambda: V.tensor_scalar(T.ibj[:], T.ibi[:], 1023, None, A.bitwise_and))
         op("v", ["ibj"], ["ib"], lambda: V.tensor_copy(T.ib[:], T.ibj[:]))
         for b in range(4):
@@ -338,7 +342,7 @@ def rank_program(g, core, T, topo):
         for b in range(4):
             mm(4 + b, "wq", "wp", 128 * b, "zq", "zp")
         wrap("fna" if last else "fow")
-        unwrap("fo", c256, 256.0, A.min)
+        unwrap("fo", "c256", c256, 256.0, A.min)
         for b in (0, 2):
             op("a", ["ps%d" % (4 + b), "hsz"], ["hs%d" % b], lambda: S.activation(T.hs[:, 272 * b:272 * b + C], bank(4 + b), F.Relu, scale=0.03125))
         for b in (1, 3):
@@ -348,10 +352,11 @@ def rank_program(g, core, T, topo):
         for b in (1, 3):
             op("v", ["hs%d" % b, "fo"], ["hg%d" % b], lambda: V.tensor_copy(T.hg[:, b:1024:4], T.hs[:, 272 * b:272 * b + C + 1].indirect(T.fo[:])))
         quant("hq", "hp", "hg", four("hg"))
+        if last:
+            gather_a(T.olr[:], "olr", T.ft[:], "ft", "fo")
+            dma("s", "dout", ["olr"], [], T.ol[:], T.olr[0:128:16, :])
         for b in range(4):
             mm(b, "eq", "ep", 128 * b, "hq", "hp", False, True)
-        if last:
-            wrap("fow")
         for b in (0, 2):
             op("a", ["ps%d" % b], ["xn%d" % b], lambda: S.activation(T.xn[:, b:1024:4], bank(b), F.Copy))
             op("v", ["ps%d" % (b + 1)], ["xn%d" % (b + 1)], lambda: V.tensor_copy(T.xn[:, b + 1:1024:4], bank(b + 1)))
@@ -360,14 +365,10 @@ def rank_program(g, core, T, topo):
     tc, tp = "tc%d" % R, "tp%d" % R
     mm(4, "vq", "vp", 0, tc, tp)
     dma("s", "dout", [tc], [], T.oc[:], view(T, tc))
-    unwrap("ola", c256, 256.0, A.min)
-    op("v", ["ola"], ["olb"], lambda: V.tensor_scalar(T.olb[:], T.ola[:], 256.0, -257.0, A.is_ge, A.mult))
     op("v", ["ps4"], ["ys"], lambda: V.tensor_copy(T.ys[:], bank(4)))
-    op("v", ["ola", "olb"], ["olc"], lambda: V.tensor_tensor(T.olc[:], T.ola[:], T.olb[:], A.add))
     for k in range(4):
         dma("a", "dout", [tp], [], T.osc[4 * k:4 * k + 4, :], T[tp][32 * k:32 * k + 4, :])
     dma("s", "dout", ["ys"], [], T.y[:], T.ys[:])
-    dma("s", "dout", ["olc"], [], T.ol[:], T.olc[:])
     g.wait_ge(T.sem.sent, sent)
     for s in sorted(count):
         need("g", (s, count[s]))

@@ -6,10 +6,12 @@ ND = 9
 BIG = float(2 ** 19)
 HUGE = float(2 ** 24)
 FAR = 2.0 ** 92
-LOW = 4096.0
+FINE = 2.0 ** -17
 PHI = 1.25 * 2.0 ** -24
 ETA = 2.0 ** -120
-X4, U8, BF, F32, U16, I32 = "float8_e4m3fn_x4", "uint8", "bfloat16", "float32", "uint16", "int32"
+BRING = (("a", 0), ("v", 1), ("a", 2), ("v", 3)), (("a", 0), ("v", 1), ("a", 2), ("v", 3))
+FETCH = (("a", 0), ("a", 1), ("a", 2), ("v", 3)), (("a", 0), ("v", 1), ("a", 2), ("v", 3))
+X4, U8, BF, F16, F32, U16, I32 = "float8_e4m3fn_x4", "uint8", "bfloat16", "float16", "float32", "uint16", "int32"
 
 
 def _s(n, d):
@@ -23,18 +25,17 @@ SCRATCH = {
     "vq": _s(128, X4), "vp": _s(128, U8), "wq": _s(512, X4), "wp": _s(512, U8), "eq": _s(512, X4), "ep": _s(512, U8),
     "nq": _s(C, X4), "np": _s(C, U8), "zq": _s(C, X4), "zp": _s(C, U8), "hq": _s(C, X4), "hp": _s(C, U8),
     "one": _s(1024, BF), "ef": _s(528, BF),
-    "pi": _s(8, I32), "pj": _s(8, I32), "col": _s(16, F32), "row": _s(C, BF), "uli": _s(32, I32), "ul": _s(32, U16), "pl": _s(16, U16),
-    "mown": _s(C, BF), "keep": _s(C, BF), "m3": _s(C, BF), "m2": _s(C, BF), "mtmp": _s(C, BF), "mfar": _s(272, BF), "msg": _s(C, BF), "mdiag": _s(C, F32),
-    "pos": _s(C, F32), "keep3": _s(768, BF), "qt": _s(1024, BF), "ft": _s(272, F32),
+    "ci": _s(48, I32), "col": _s(16, F32), "row": _s(C, BF), "ul": _s(32, U16), "pl": _s(16, U16),
+    "mown": _s(C, BF), "keep": _s(C, BF), "m3": _s(C, BF), "mfar": _s(272, BF), "msg": _s(C, BF),
+    "mdiag": _s(C, F32), "pos": _s(C, F32), "keep3": _s(768, BF), "mfine": _s(C, F32), "step": _s(C, F32), "ft": _s(272, F32),
     "mk": _s(C, F32), "hold": _s(C, F32), "dl": _s(C, BF), "dw": _s(16, F32), "t3": _s(C, BF), "rb": _s(288, F32),
     "sgo": _s(768, BF), "vv": _s(768, BF), "pay": _s(C, F32),
-    "cm": _s(272 * ND, BF), "sc": _s(136 * ND, BF), "sa": _s(272 * (16 - ND), BF),
-    "rk": _s(16, F32), "rko": _s(16, U16), "vsd": _s(C, F32), "cb": _s(C, F32), "cbh": _s(C, BF),
-    "lo": _s(16, U16), "lp": _s(16, U16),
-    "qr": _s(C, BF), "sto": _s(264, F32), "stp": _s(264, F32), "aown": _s(16, U16), "apar": _s(16, U16),
+    "cm": _s(272 * ND, BF), "sc": _s(136 * ND + 136, F16), "sa": _s(272 * (16 - ND), BF),
+    "rk": _s(16, F32), "rko": _s(16, U16), "vsd": _s(C, F32), "cb": _s(C, F32), "cbh": _s(C, BF), "cb2": _s(C, F32),
+    "lo": _s(16, U16), "lp": _s(16, U16), "oi": _s(64, I32), "sto": _s(264, F32),
     "wm": _s(1024, BF), "wm2": _s(1024, BF), "seg": _s(1024, BF), "fpr": _s(C, BF), "fsr": _s(C, BF), "fow": _s(C, BF), "fna": _s(C, BF),
     "fpo": _s(16, U16), "bv": _s(C, F32), "wsg": _s(512, F32), "cum": _s(C, F32),
-    "ia": _s(16, U16), "ib": _s(16, U16), "ibi": _s(16, I32), "ibj": _s(16, I32), "fo": _s(16, U16), "olr": _s(C, F32),
+    "ia": _s(16, U16), "ib": _s(16, U16), "ibi": _s(32, I32), "fo": _s(16, U16), "olr": _s(C, F32),
     "do": _s(1024, BF), "dp": _s(1024, BF), "dos": _s(1024, BF), "dps": _s(1024, BF), "tmp": _s(1024, BF),
     "z": _s(1024, BF), "hs": _s(272 * 4, BF), "hg": _s(1024, BF), "xn": _s(1024, BF), "ys": _s(C, F32),
     "ps": ("psum", [128, 4096], F32),
@@ -43,13 +44,14 @@ for _t in range(R + 1):
     SCRATCH["tc%d" % _t] = _s(C, X4)
     SCRATCH["tp%d" % _t] = _s(C, U8)
 for _t in range(R):
-    for _n, _w, _d in (("c", C, X4), ("p", C, U8), ("l", 16, U16)):
+    for _n, _w, _d in (("c", C, X4), ("p", C, U8), ("l", 16, U16), ("o", 8, U16)):
         SCRATCH["hop%s%d" % (_n, _t)] = _s(_w, _d)
         SCRATCH["far%s%d" % (_n, _t)] = _s(_w, _d)
     SCRATCH["ls%d" % _t] = _s(16, U16)
+    SCRATCH["lt%d" % _t] = _s(8, U16)
 
 SEMAPHORES = ["cv", "ca", "cp", "cg", "dx", "du", "dv", "dwc", "dws", "dout", "sent"] + \
-    ["a%s%d" % (n, t) for n in "cpl" for t in range(R)]
+    ["a%s%d" % (n, t) for n in "cplo" for t in range(R)]
 
 
 def relays(T, topo, rank):
@@ -89,7 +91,7 @@ def rank_program(g, core, T, topo):
             if core == a:
                 relay_program(g, core, T, topo, r, "pl")
             if core == b:
-                relay_program(g, core, T, topo, r, "c")
+                relay_program(g, core, T, topo, r, "co")
         return
     ra, rb_ = relays(T, topo, rank)
     Q = {"v": g.vector, "a": g.scalar, "p": g.tensor, "g": g, "s": g.sync}
@@ -142,38 +144,37 @@ def rank_program(g, core, T, topo):
     def four(name):
         return ["%s%d" % (name, b) for b in range(4)]
 
-    def mm(b, lq, lp, a, rq, rp, start=True, stop=True):
-        op("p", [lq, rq, lp, rp], ["ps%d" % b], lambda: PE.matmul_mx(
-            bank(b), T[lq][:, a:a + 128], T[lp][:, a:a + 128], T[rq][:], T[rp][:], start, stop))
+    def keys(name):
+        return [name, name + "/0", name + "/1"]
+
+    def mm(b, lq, lp, a, rq, rp, start=True, stop=True, h=None):
+        lo, n = (0, C) if h is None else (128 * h, 128)
+        rd = keys(rq) if h is None else [rq, "%s/%d" % (rq, h)]
+        op("p", [lq, lp, rp] + rd, ["ps%d" % b], lambda: PE.matmul_mx(
+            bank(b, n), T[lq][:, a:a + 128], T[lp][:, a:a + 128], T[rq][:, lo:lo + n], T[rp][:, lo:lo + n], start, stop))
 
     def quant(q, p, src, rd):
         op("v", rd, [q, p], lambda: V.quantize_mx(T[q][:], T[p][:], T[src][:]))
 
+    def quant_half(q, p, src, rd, h):
+        op("v", rd, ["%s/%d" % (q, h)], lambda: V.quantize_mx(part(q, h, 128), part(p, h, 128), part(src, h, 512)))
+
     def pick(q2, p2, q, p, key, off):
-        op("v", [q, key], [q2], lambda: V.tensor_copy(T[q2][:].bitcast(dt.uint32), T[q][:].bitcast(dt.uint32).indirect(off)))
-        op("a", [p, key], [p2], lambda: S.activation(T[p2][:], T[p][:].indirect(off), F.Copy))
+        op("v", keys(q) + [key], [q2], lambda: V.tensor_copy(T[q2][:].bitcast(dt.uint32), T[q][:].bitcast(dt.uint32).indirect(off)))
+        op("a", keys(q) + [p, key], [p2], lambda: S.activation(T[p2][:], T[p][:].indirect(off), F.Copy))
 
-    def wrap(name):
-        op("v", ["mdiag", name], ["cb"], lambda: V.tensor_tensor_scan(T.cb[:], T.mdiag[:], T[name][:, 0:C], 0.0, A.add, A.max))
+    def wrap(name, mask="mdiag", out="cb"):
+        op("v", [mask, name], [out], lambda: V.tensor_tensor_scan(T[out][:], T[mask][:], T[name][:, 0:C], 0.0, A.add, A.max))
 
-    ends = T.cb[:, 15:C:16]
-    c0, c256, c1024, clist, cplace, pm, pm16, pmh = (T.col[:, j:j + 1] for j in range(8))
+    c0, c256, c1024, cfine, pm, pm16, pmh = (T.col[:, j:j + 1] for j in range(7))
+    oi, oj, ok, om, ri, rj = T.oi[:, 0:16], T.oi[:, 16:32], T.oi[:, 32:40], T.oi[:, 40:48], T.oi[:, 48:56], T.oi[:, 56:64]
+    ibi, ibj = T.ibi[:, 0:16], T.ibi[:, 16:32]
 
-    def unwrap(out, key, s1, s2=None, op1=None):
-        if s2 is None:
-            op("v", ["cb", key], [out], lambda: V.tensor_scalar(T[out][:], ends, s1, None, A.add))
-        else:
-            op("v", ["cb", key], [out], lambda: V.tensor_scalar(T[out][:], ends, s1, s2, A.add, op1))
+    def unwrap(key, out, ckey, s1, s2, op1, src="cb"):
+        op("v", [src, ckey], [key], lambda: V.tensor_scalar(out, T[src][:, 15:C:16], s1, s2, A.add, op1))
 
     def signs(m):
         op("a", ["ps%d" % (2 + m)], ["sgo%d" % m], lambda: S.activation(T.sgo[:, m:768:3], bank(2 + m), F.Sign, bias=-ETA))
-
-    def starts(lst, st, out, between):
-        op("v", ["qt", lst], ["qr"], lambda: V.tensor_copy(T.qr[:], T.qt[:].indirect(T[lst][:])))
-        between()
-        op("v", ["qr"], [st], lambda: V.tensor_tensor_scan(T[st][:, 1:C + 1], T.qr[:], T.qr[:], 0.0, A.add, A.max))
-        wrap(st)
-        unwrap(out, "c0", c0)
 
     def gather_a(out, okey, win, wkey, off):
         op("a", [wkey, off], [okey], lambda: S.activation(out, win.indirect(T[off][:]), F.Copy))
@@ -181,33 +182,37 @@ def rank_program(g, core, T, topo):
     def iota(key, pattern, base, out=None):
         op("g", [], [key], lambda: g.iota(T[key][:] if out is None else out, pattern, base, 0, allow_small_or_imprecise_dtypes=True))
 
-    def column(key, out, add):
-        op("a", ["c0"], [key], lambda: S.activation(out, c0, F.Identity, bias=add))
+    def line(key, out, rd, in_, scale, bias):
+        op("a", [rd], [key], lambda: S.activation(out, in_, F.Identity, bias=bias, scale=scale))
 
     dma("s", "dx", [], ["xs"], T.xs[:], T.x[:])
     dma("a", "du", [], ["us"], T.us[:], T.u[:])
     op("v", [], ["one"], lambda: V.memset(T.one[:], 1.0))
-    op("g", [], ["pi"], lambda: g.iota(T.pi[:], [[0, 8]], 0, 1))
-    op("g", [], ["uli"], lambda: g.iota(T.uli[:], [[1, 4], [16, 8]], 0, 0))
+    op("g", [], ["pi"], lambda: g.iota(T.ci[:, 32:40], [[0, 8]], 0, 1))
+    op("g", [], ["uli"], lambda: g.iota(T.ci[:, 0:32], [[1, 4], [16, 8]], 0, 0))
     iota("row", [[0, 16], [1, 16]], 0)
     op("g", ["one"], ["ef"], lambda: g.affine_select(T.ef[:], T.one[:, 0:528], [[-1, 528]], A.is_equal, 0.0, 3, 4))
-    iota("pos", [[8, C]], 3 - int(LOW))
-    op("v", ["pi"], ["pj"], lambda: V.tensor_scalar(T.pj[:], T.pi[:], 15, None, A.bitwise_and))
-    op("v", ["uli"], ["ul"], lambda: V.tensor_copy(T.ul[:], T.uli[:]))
-    op("v", ["pj"], ["pm"], lambda: V.tensor_copy(pm, T.pj[:, 0:1]))
+    iota("pay", [[1, C]], 0)
+    op("v", ["pi"], ["pj"], lambda: V.tensor_scalar(T.ci[:, 40:48], T.ci[:, 32:40], 15, None, A.bitwise_and))
+    op("v", ["uli"], ["ul"], lambda: V.tensor_copy(T.ul[:], T.ci[:, 0:32]))
+    op("v", ["pj"], ["pm"], lambda: V.tensor_copy(pm, T.ci[:, 40:41]))
     op("v", [], ["mfz"], lambda: V.memset(T.mfar[:, 0:16], 0.0))
-    op("a", ["pm"], ["pmh"], lambda: S.activation(pmh, pm, F.Identity, bias=-0.5, scale=-1.0))
-    op("a", ["pm"], ["pm16"], lambda: S.activation(pm16, pm, F.Copy, scale=16.0))
-    op("a", ["pm"], ["c0"], lambda: S.activation(c0, pm, F.Identity, bias=-15.0 * BIG, scale=BIG))
+    line("pmh", pmh, "pm", pm, -1.0, -0.5)
+    line("pm16", pm16, "pm", pm, 16.0, 0.0)
+    line("c0", c0, "pm", pm, BIG, -15.0 * BIG)
+    op("v", ["pm"], ["scz"], lambda: V.tensor_scalar(T.sc[:, 135:136], pm, 0.0, -1024.0, A.mult, A.add))
     op("v", ["row", "pm"], ["mown"], lambda: V.tensor_scalar(T.mown[:], T.row[:], pm, None, A.is_equal))
-    op("v", ["row", "pm"], ["mtmp"], lambda: V.tensor_scalar(T.mtmp[:], T.row[:], pm, 4 * FAR, A.is_lt, A.mult))
+    op("v", ["row", "pm"], ["dl"], lambda: V.tensor_scalar(T.dl[:], T.row[:], pm, 4 * FAR, A.is_lt, A.mult))
     op("v", ["row"], ["keep"], lambda: V.tensor_scalar(T.keep[:], T.row[:], 0.0, None, A.is_gt))
     op("v", ["row", "pm16"], ["pl"], lambda: V.tensor_scalar(T.pl[:], T.row[:, 0:16], pm16, None, A.add))
-    op("a", ["mown"], ["mfar"], lambda: S.activation(T.mfar[:, 16:272], T.mown[:], F.Copy, scale=FAR))
+    line("mfar", T.mfar[:, 16:272], "mown", T.mown[:], FAR, 0.0)
     op("a", ["row", "pmh"], ["msg"], lambda: S.activation(T.msg[:], T.row[:], F.Sign, bias=pmh))
-    op("a", ["msg"], ["mdiag"], lambda: S.activation(T.mdiag[:], T.msg[:], F.Identity, bias=(BIG - HUGE) / 2, scale=(BIG + HUGE) / 2))
-    op("v", ["mfar", "mfz"], ["m2"], lambda: V.tensor_tensor(T.m2[:], T.mfar[:, 15:271], T.mfar[:, 16:272], A.subtract))
-    op("v", ["m2", "mtmp"], ["m3"], lambda: V.tensor_tensor(T.m3[:], T.mtmp[:], T.m2[:], A.add))
+    line("mdiag", T.mdiag[:], "msg", T.msg[:], (BIG + HUGE) / 2, (BIG - HUGE) / 2)
+    line("mfine", T.mfine[:], "msg", T.msg[:], 132.0, -124.0)
+    line("pos", T.pos[:], "pay", T.pay[:], FINE, -8.0)
+    line("cfine", cfine, "pm", pm, 8.0, -108.0)
+    op("v", ["mfar", "mfz"], ["t3"], lambda: V.tensor_tensor(T.t3[:], T.mfar[:, 15:271], T.mfar[:, 16:272], A.subtract))
+    op("v", ["t3", "dl"], ["m3"], lambda: V.tensor_tensor(T.m3[:], T.dl[:], T.t3[:], A.add))
     quant("uq", "up", "us", ["us"])
     pick("u1q", "u1p", "uq", "up", "ul", T.ul[:, 0:8])
     quant("q0", "p0", "xs", ["xs"])
@@ -218,22 +223,20 @@ def rank_program(g, core, T, topo):
     for t in range(R):
         buys = not rank >> t & 1
         last = t == R - 1
-        tc, tp, ls = "tc%d" % t, "tp%d" % t, "ls%d" % t
-        fc, fp, fl = "farc%d" % t, "farp%d" % t, "farl%d" % t
+        tc, tp, ls, lt = "tc%d" % t, "tp%d" % t, "ls%d" % t, "lt%d" % t
+        fc, fp, fl, fo_ = "farc%d" % t, "farp%d" % t, "farl%d" % t, "faro%d" % t
         partner = T.cores[rank ^ (1 << t)]
-        last_w[fc] = ("ac%d" % t, len(topo.engines(rb_, partner)))
-        last_w[fp] = ("ap%d" % t, len(topo.engines(ra, partner)))
-        last_w[fl] = ("al%d" % t, len(topo.engines(ra, partner)))
-        order("g", [tc], [])
+        for key, sem, relay in ((fc, "ac", rb_), (fp, "ap", ra), (fl, "al", ra), (fo_, "ao", rb_)):
+            last_w[key] = ("%s%d" % (sem, t), len(topo.engines(relay, partner)))
+        order("g", keys(tc), [])
         sent += write(g, T, topo, core, rb_, "hopc%d" % t, tc, "ac%d" % t)
         order("g", [tp], [])
         sent += write(g, T, topo, core, ra, "hopp%d" % t, tp, "ap%d" % t)
         if t == 0:
             op("g", ["one"], ["keep3"], lambda: g.affine_select(T.keep3[:], T.one[:, 0:768], [[0, C], [1, 3]], A.is_gt, 0.0, 0, 0))
-            iota("qt", [[0, C], [1, 4]], 1)
+            iota("step", [[0, C]], 13)
             iota("sto", [[0, 8]], 0, T.sto[:, 0:8])
-        else:
-            iota("wsg", [[0, 512]], 1)
+        iota("wsg", [[0, 512]], 1)
         iota("wm", [[0, 1024]], 0)
         mm(0, "u1q", "u1p", 0, tc, tp)
         mm(1, "u1q", "u1p", 0, tc, tp)
@@ -265,75 +268,81 @@ def rank_program(g, core, T, topo):
         for k in range(ND, 16):
             op("a", ["sa%d" % k], ["sa%d" % k, "rk%d" % k], lambda: S.activation(
                 part("sa", k - ND, 272), part("sa", k - ND, 272), F.Relu, scale=-1.0, accum_out=T.rk[:, k:k + 1]))
+        op("v", ["cm%d" % k for k in range(ND)], ["sc"], lambda: V.tensor_tensor_scan(
+            T.sc[:, 136:], T.cm[:, 0:272 * ND:2], T.cm[:, 1:272 * ND:2], -1024.0, A.add, A.add))
+        if t == 0:
+            line("c256", c256, "c0", c0, 1.0, 256.0)
+            line("c1024", c1024, "c0", c0, 1.0, -1024.0)
         op("v", ["sgo0", "sgo1", "sgo2", "keep3"], ["vv"], lambda: V.tensor_tensor_scan(T.vv[:], T.keep3[:], T.sgo[:], 0.0, A.mult, A.add))
-        for k in range(ND):
-            op("v", ["cm%d" % k], ["sc%d" % k], lambda: V.tensor_tensor_scan(
-                part("sc", k, 136), part("cm", 2 * k, 136), part("cm", 2 * k + 1, 136), 0.0, A.add, A.add))
-        op("v", ["vv", "pos"], ["pay"], lambda: V.tensor_tensor_scan(T.pay[:], T.vv[:, 2:768:3], T.pos[:], -LOW, A.max, A.add))
+        op("v", ["sc", "scz"], ["rkv"], lambda: V.tensor_tensor(
+            T.rk[:, 0:ND], T.sc[:, 271:136 * ND + 136:136], T.sc[:, 135:136 * ND:136], A.subtract))
+        op("v", ["vv", "pos"], ["pay"], lambda: V.tensor_tensor_scan(T.pay[:], T.vv[:, 2:768:3], T.pos[:], -8.0, A.max, A.add))
         if t == 0:
-            column("clist", clist, LOW)
-            column("cplace", cplace, LOW - 3.0)
-            column("c256", c256, 256.0)
-            column("c1024", c1024, -1024.0)
-        op("v", ["sc%d" % k for k in range(ND)], ["rkv"], lambda: V.tensor_scalar(T.rko[:, 0:ND], T.sc[:, 135:136 * ND:136], 0.0, None, A.add))
-        op("v", ["rk%d" % k for k in range(ND, 16)], ["rko"], lambda: V.tensor_copy(T.rko[:, ND:16], T.rk[:, ND:16]))
-        op("v", ["pay", "rkv", "rko"], ["vsd"], lambda: V.tensor_copy(T.vsd[:].indirect(T.rko[:]), T.pay[:]))
-        wrap("vsd")
-        unwrap(ls, "clist", clist, 0.5, A.mult)
-        order("g", [ls], [])
-        sent += write(g, T, topo, core, ra, "hopl%d" % t, ls, "al%d" % t)
-        if t == 0:
-            iota("stp", [[0, 8]], 0, T.stp[:, 0:8])
-            iota("wsg", [[0, 512]], 1)
             for b in range(4):
                 op("v", ["ef"], ["eq", "ep"] if b == 3 else ["eq%d" % b], lambda: V.quantize_mx(
                     part("eq", b, 128), part("ep", b, 128), T.ef[:, 3 - b:515 - b]))
+        op("v", ["rkv"] + ["rk%d" % k for k in range(ND, 16)], ["rko"], lambda: V.tensor_copy(T.rko[:], T.rk[:]))
+        op("v", ["pay", "rko"], ["vsd"], lambda: V.tensor_copy(T.vsd[:].indirect(T.rko[:]), T.pay[:]))
+        op("v", ["vsd", "step"], ["sto"], lambda: V.tensor_tensor_scan(T.sto[:, 1:C + 1], T.vsd[:], T.step[:], 0.0, A.add, A.add))
+        wrap("vsd", "mfine", "cb2")
+        wrap("sto")
+        unwrap("oi", oi, "cfine", cfine, 1.0 / FINE, A.mult, "cb2")
+        unwrap(ls, T[ls][:], "c0", c0, 0.5, A.mult)
+        order("g", [ls], [])
+        sent += write(g, T, topo, core, ra, "hopl%d" % t, ls, "al%d" % t)
         for b in range(4):
             mm(b, "eq", "ep", 128 * b, tc, tp)
         for b in range(4):
             mm(4 + b, "eq", "ep", 128 * b, fc, fp)
         for b in range(4):
             op("a", ["ps%d" % b], ["do%d" % b], lambda: S.activation(part("do", b), bank(b), F.Copy, scale=0.5))
-        unwrap("lo", "cplace", cplace, 0.125, A.mult)
-        starts(ls, "sto", "aown", lambda: None)
-        op("v", ["one", "aown"], ["wm"], lambda: V.tensor_copy(T.wm[:].indirect(T.aown[:]), T.one[:, 0:C]))
-        op("g", ["wm"], ["wm2"], lambda: g.affine_select(T.wm2[:], T.wm[:], [[0, 1024]], A.is_gt, 0.0, 1, 0))
+        for b in range(4):
+            op("a", ["ps%d" % (4 + b)], ["dp%d" % b], lambda: S.activation(part("dp", b), bank(4 + b), F.Copy, scale=0.5))
+        op("v", ["oi"], ["oj"], lambda: V.tensor_scalar(oj, oi, 255, None, A.bitwise_and))
+        op("v", ["oj"], ["lo"], lambda: V.tensor_copy(T.lo[:], oj))
+        for b in range(4):
+            gather_a(part("dos", b), "dos%d" % b, part("do", b), "do%d" % b, "lo")
+        op("v", ["oj"], ["ok"], lambda: V.tensor_scalar(ok, T.oi[:, 16:24], 256.0, None, A.mult))
+        op("v", ["oj", "ok"], ["om"], lambda: V.tensor_tensor(om, ok, T.oi[:, 24:32], A.add))
+        op("v", ["om"], [lt], lambda: V.tensor_copy(T[lt][:], om))
+        order("g", [lt], [])
+        sent += write(g, T, topo, core, rb_, "hopo%d" % t, lt, "ao%d" % t)
         if t == 0:
             iota("hsz", [[0, 4]], 0, T.hs[:, C:272 * 4:272])
+        op("v", ["one", ls], ["wm"], lambda: V.tensor_copy(T.wm[:].indirect(T[ls][:]), T.one[:, 0:C]))
+        op("v", ["wm"], ["wm2"], lambda: V.tensor_copy(T.wm2[:], T.wm[:]))
         if t == 1:
             iota("ft", [[1, 272]], 0)
             iota("ft", [[0, 8]], -1, T.ft[:, C:C + 8])
             quant("vq", "vp", "vs", ["vs"])
-        for b in range(4):
-            op("a", ["ps%d" % (4 + b)], ["dp%d" % b], lambda: S.activation(part("dp", b), bank(4 + b), F.Copy, scale=0.5))
         if last:
             pick("nq", "np", tc, tp, "pl", T.pl[:])
+        dq, dp_ = ("nq", "np") if last else (tc, tp)
         for b in range(4):
-            mm(b, "eq", "ep", 128 * b, "nq" if last else tc, "np" if last else tp, True, False)
-        for b in range(4):
-            gather_a(part("dos", b), "dos%d" % b, part("do", b), "do%d" % b, "lo")
-        starts(fl, "stp", "apar", lambda: op("v", [fl], ["lp"], lambda: V.tensor_scalar(T.lp[:], T[fl][:], 0.25, -0.375, A.mult, A.add)))
-        for b in range(2):
-            gather_a(part("dps", b), "dps%d" % b, part("dp", b), "dp%d" % b, "lp")
-        op("a", ["wm2", "apar"], ["bv"], lambda: S.activation(T.bv[:], T.wm2[:].indirect(T.apar[:]), F.Identity, bias=1024.0))
-        for b in range(2, 4):
-            gather_a(part("dps", b), "dps%d" % b, part("dp", b), "dp%d" % b, "lp")
-        op("v", ["one", "apar"], ["wm"], lambda: V.tensor_copy(T.wm[:].indirect(T.apar[:]), T.one[:, 0:C]))
+            mm(b, "eq", "ep", 128 * b, dq, dp_, True, False, 0)
+        op("v", ["one", fl], ["wm"], lambda: V.tensor_copy(T.wm[:].indirect(T[fl][:]), T.one[:, 0:C]))
+        op("a", ["wm2", fl], ["bv"], lambda: S.activation(T.bv[:], T.wm2[:].indirect(T[fl][:]), F.Identity, bias=1024.0))
         op("v", ["wm", "one"], ["seg"], lambda: V.tensor_tensor_scan(T.seg[:], T.one[:], T.wm[:], -257.0, A.mult, A.add))
-        op("v", ["seg", "apar", "mown"], ["fpr"], lambda: V.tensor_tensor(T.fpr[:], T.seg[:].indirect(T.apar[:]), T.mown[:], A.mult))
-        gather_a(T.fsr[:], "fsr", T.seg[:], "seg", "aown")
-        op("a", ["fsr", "rko", "rkv"], ["fow"], lambda: S.activation(T.fow[:], T.fsr[:].indirect(T.rko[:]), F.Copy))
+        op("v", [fo_], ["ri"], lambda: V.tensor_copy(ri, T[fo_][:]))
+        op("v", ["seg", fl, "mown"], ["fpr"], lambda: V.tensor_tensor(T.fpr[:], T.seg[:].indirect(T[fl][:]), T.mown[:], A.mult))
+        gather_a(T.fsr[:], "fsr", T.seg[:], "seg", ls)
+        gather_a(T.fow[:], "fow", T.fsr[:], "fsr", "rko")
         if last:
             gather_a(T.fna[:], "fna", T.fow[:], "fow", "pl")
+        op("v", ["ri"], ["rj"], lambda: V.tensor_scalar(rj, ri, 255, None, A.bitwise_and))
         op("v", ["fpr", "keep"], ["cbh"], lambda: V.tensor_tensor_scan(T.cbh[:], T.keep[:], T.fpr[:], 0.0, A.mult, A.add))
+        op("v", [fo_], ["lp0"], lambda: V.tensor_scalar(T.lp[:, 0:8], T[fo_][:], 1.0 / 256, -0.498046875, A.mult, A.add))
         op("v", ["cbh"], ["fpo"], lambda: V.tensor_scalar(T.fpo[:], T.cbh[:, 15:C:16], 256.0, None, A.add))
+        op("v", ["rj", "lp0"], ["lp"], lambda: V.tensor_copy(T.lp[:, 8:16], rj))
+        for b in range(4):
+            gather_a(part("dps", b), "dps%d" % b, part("dp", b), "dp%d" % b, "lp")
         op("v", ["bv", "fpo"], ["wsg"], lambda: V.tensor_copy(T.wsg[:].indirect(T.fpo[:]), T.bv[:]))
         op("v", ["wsg"], ["cum"], lambda: V.tensor_tensor_scan(T.cum[:], T.wsg[:, 0:C], T.wsg[:, 0:C], 0.0, A.add, A.max))
         wrap("cum")
-        unwrap("ia", "c1024", c1024, 1.0 / 1024, A.mult)
-        unwrap("ibi", "c0", c0, -1.0, A.add)
-        op("v", ["ibi"], ["ibj"], lambda: V.tensor_scalar(T.ibj[:], T.ibi[:], 1023, None, A.bitwise_and))
-        op("v", ["ibj"], ["ib"], lambda: V.tensor_copy(T.ib[:], T.ibj[:]))
+        unwrap("ia", T.ia[:], "c1024", c1024, 1.0 / 1024, A.mult)
+        unwrap("ibi", ibi, "c0", c0, -1.0, A.add)
+        op("v", ["ibi"], ["ibj"], lambda: V.tensor_scalar(ibj, ibi, 1023, None, A.bitwise_and))
+        op("v", ["ibj"], ["ib"], lambda: V.tensor_copy(T.ib[:], ibj))
         for b in range(4):
             gather_a(part("tmp", b), "tmp%d" % b, part("dps", b), "dps%d" % b, "ia")
             op("v", ["dos%d" % b, "ib", "tmp%d" % b], ["z%d" % b], lambda: V.tensor_tensor(
@@ -342,33 +351,47 @@ def rank_program(g, core, T, topo):
         for b in range(4):
             mm(4 + b, "wq", "wp", 128 * b, "zq", "zp")
         wrap("fna" if last else "fow")
-        unwrap("fo", "c256", c256, 256.0, A.min)
+        unwrap("fo", T.fo[:], "c256", c256, 256.0, A.min)
         for b in (0, 2):
             op("a", ["ps%d" % (4 + b), "hsz"], ["hs%d" % b], lambda: S.activation(T.hs[:, 272 * b:272 * b + C], bank(4 + b), F.Relu, scale=0.03125))
         for b in (1, 3):
             op("v", ["ps%d" % (4 + b), "hsz"], ["hs%d" % b], lambda: V.tensor_scalar(T.hs[:, 272 * b:272 * b + C], bank(4 + b), 0.0, 0.03125, A.max, A.mult))
-        for b in (0, 2):
-            gather_a(T.hg[:, b:1024:4], "hg%d" % b, T.hs[:, 272 * b:272 * b + C + 1], "hs%d" % b, "fo")
-        for b in (1, 3):
-            op("v", ["hs%d" % b, "fo"], ["hg%d" % b], lambda: V.tensor_copy(T.hg[:, b:1024:4], T.hs[:, 272 * b:272 * b + C + 1].indirect(T.fo[:])))
-        quant("hq", "hp", "hg", four("hg"))
-        if last:
-            gather_a(T.olr[:], "olr", T.ft[:], "ft", "fo")
-            dma("s", "dout", ["olr"], [], T.ol[:], T.olr[0:128:16, :])
         for b in range(4):
-            mm(b, "eq", "ep", 128 * b, "hq", "hp", False, True)
-        for b in (0, 2):
-            op("a", ["ps%d" % b], ["xn%d" % b], lambda: S.activation(T.xn[:, b:1024:4], bank(b), F.Copy))
-            op("v", ["ps%d" % (b + 1)], ["xn%d" % (b + 1)], lambda: V.tensor_copy(T.xn[:, b + 1:1024:4], bank(b + 1)))
-        quant("tc%d" % (t + 1), "tp%d" % (t + 1), "xn", four("xn"))
+            mm(4 + b, "eq", "ep", 128 * b, dq, dp_, True, False, 1)
+        nq, np_ = "tc%d" % (t + 1), "tp%d" % (t + 1)
+
+        def bring(q, b, h):
+            out, win, off = T.hg[:, 512 * h + b:512 * h + 512:4], T.hs[:, 272 * b:272 * b + C + 1], T.fo[:, 8 * h:8 * h + 8]
+            op(q, ["hs%d" % b, "fo"], ["hg%d%d" % (b, h)], (lambda: V.tensor_copy(out, win.indirect(off))) if q == "v" else (
+                lambda: S.activation(out, win.indirect(off), F.Copy)))
+
+        def fetch(q, key, out, b):
+            op(q, ["ps%d" % b], [key], (lambda: V.tensor_copy(out, bank(b, 128))) if q == "v" else (
+                lambda: S.activation(out, bank(b, 128), F.Copy)))
+
+        for h in range(2):
+            for q, b in BRING[h]:
+                bring(q, b, h)
+            quant_half("hq", "hp", "hg", ["hg%d%d" % (b, h) for b in range(4)], h)
+            for b in range(4):
+                mm(4 * h + b, "eq", "ep", 128 * b, "hq", "hp", False, True, h)
+        for h in range(2):
+            for q, b in FETCH[h]:
+                fetch(q, "xn%d%d" % (b, h), T.xn[:, 512 * h + b:512 * h + 512:4], 4 * h + b)
+            quant_half(nq, np_, "xn", ["xn%d%d" % (b, h) for b in range(4)], h)
+            if last:
+                mm(4 * h, "vq", "vp", 0, nq, np_, True, True, h)
+                dma("s", "dout", ["%s/%d" % (nq, h)], [], part("oc", h, 512), part(nq, h, 128).bitcast(dt.uint8))
 
     tc, tp = "tc%d" % R, "tp%d" % R
-    mm(4, "vq", "vp", 0, tc, tp)
-    dma("s", "dout", [tc], [], T.oc[:], view(T, tc))
-    op("v", ["ps4"], ["ys"], lambda: V.tensor_copy(T.ys[:], bank(4)))
+    fetch("a", "ys0", part("ys", 0, 128), 0)
+    dma("s", "dout", ["ys0"], [], part("y", 0, 128), part("ys", 0, 128))
+    gather_a(T.olr[:], "olr", T.ft[:], "ft", "fo")
+    fetch("v", "ys1", part("ys", 1, 128), 4)
+    dma("s", "dout", ["ys1"], [], part("y", 1, 128), part("ys", 1, 128))
+    dma("a", "dout", ["olr"], [], T.ol[:], T.olr[0:128:16, :])
     for k in range(4):
-        dma("a", "dout", [tp], [], T.osc[4 * k:4 * k + 4, :], T[tp][32 * k:32 * k + 4, :])
-    dma("s", "dout", ["ys"], [], T.y[:], T.ys[:])
+        dma("a", "dout", keys(tc), [], T.osc[4 * k:4 * k + 4, :], T[tp][32 * k:32 * k + 4, :])
     g.wait_ge(T.sem.sent, sent)
     for s in sorted(count):
         need("g", (s, count[s]))

from concourse.mybir import dt, AluOpType as A, ActivationFunctionType as F

C = 256
R = 3
ND = 9
BIG = float(2 ** 19)
HUGE = float(2 ** 24)
FAR = 2.0 ** 92
FINE = 2.0 ** -17
PHI = 1.25 * 2.0 ** -24
ETA = 2.0 ** -120
BRING = (("a", 0), ("v", 1), ("a", 2), ("v", 3)), (("a", 0), ("v", 1), ("a", 2), ("v", 3))
FETCH = (("a", 0), ("a", 1), ("a", 2), ("v", 3)), (("a", 0), ("v", 1), ("a", 2), ("v", 3))
X4, U8, BF, F16, F32, U16, I32 = "float8_e4m3fn_x4", "uint8", "bfloat16", "float16", "float32", "uint16", "int32"


def _s(n, d):
    return ("sbuf", [128, n], d)


SCRATCH = {
    "xs": _s(1024, BF), "us": _s(512, BF), "vs": _s(512, BF),
    "q0": _s(C, X4), "p0": _s(C, U8), "uq": _s(128, X4), "up": _s(128, U8), "u1q": _s(128, X4), "u1p": _s(128, U8),
    "u3q": _s(384, X4), "u3p": _s(384, U8),
    "vq": _s(128, X4), "vp": _s(128, U8), "wq": _s(512, X4), "wp": _s(512, U8), "eq": _s(512, X4), "ep": _s(512, U8),
    "nq": _s(C, X4), "np": _s(C, U8), "zq": _s(C, X4), "zp": _s(C, U8), "hq": _s(C, X4), "hp": _s(C, U8),
    "one": _s(1024, BF), "ef": _s(528, BF),
    "ci": _s(48, I32), "col": _s(16, F32), "row": _s(C, BF), "ul": _s(32, U16), "pl": _s(16, U16),
    "mown": _s(C, BF), "keep": _s(C, BF), "m3": _s(C, BF), "mfar": _s(272, BF), "msg": _s(C, BF),
    "mdiag": _s(C, F32), "pos": _s(C, F32), "keep3": _s(768, BF), "mfine": _s(C, F32), "step": _s(C, F32), "ft": _s(272, F32),
    "mk": _s(C, F32), "hold": _s(C, F32), "dl": _s(C, BF), "dw": _s(16, F32), "t3": _s(C, BF), "rb": _s(288, F32),
    "sgo": _s(768, BF), "vv": _s(768, BF), "pay": _s(C, F32),
    "cm": _s(272 * ND, BF), "sc": _s(136 * ND + 136, F16), "sa": _s(272 * (16 - ND), BF),
    "rk": _s(16, F32), "rko": _s(16, U16), "vsd": _s(C, F32), "cb": _s(C, F32), "cbh": _s(C, BF), "cb2": _s(C, F32),
    "lo": _s(16, U16), "lp": _s(16, U16), "oi": _s(64, I32), "sto": _s(264, F32),
    "wm": _s(1024, BF), "wm2": _s(1024, BF), "seg": _s(1024, BF), "fpr": _s(C, BF), "fsr": _s(C, BF), "fow": _s(C, BF), "fna": _s(C, BF),
    "fpo": _s(16, U16), "bv": _s(C, F32), "wsg": _s(512, F32), "cum": _s(C, F32),
    "ia": _s(16, U16), "ib": _s(16, U16), "ibi": _s(32, I32), "fo": _s(16, U16), "olr": _s(C, F32),
    "do": _s(1024, BF), "dp": _s(1024, BF), "dos": _s(1024, BF), "dps": _s(1024, BF), "tmp": _s(1024, BF),
    "z": _s(1024, BF), "hs": _s(272 * 4, BF), "hg": _s(1024, BF), "xn": _s(1024, BF), "ys": _s(C, F32),
    "ps": ("psum", [128, 4096], F32),
}
for _t in range(R + 1):
    SCRATCH["tc%d" % _t] = _s(C, X4)
    SCRATCH["tp%d" % _t] = _s(C, U8)
for _t in range(R):
    for _n, _w, _d in (("c", C, X4), ("p", C, U8), ("l", 16, U16), ("o", 8, U16)):
        SCRATCH["hop%s%d" % (_n, _t)] = _s(_w, _d)
        SCRATCH["far%s%d" % (_n, _t)] = _s(_w, _d)
    SCRATCH["ls%d" % _t] = _s(16, U16)
    SCRATCH["lt%d" % _t] = _s(8, U16)

SEMAPHORES = ["cv", "ca", "cp", "cg", "dx", "du", "dv", "dwc", "dws", "dout", "sent"] + \
    ["a%s%d" % (n, t) for n in "cplo" for t in range(R)]


def relays(T, topo, rank):
    me = T.cores[rank]
    far = [T.cores[rank ^ (1 << t)] for t in range(R)]
    ok = [c for c in topo.cores_of(me) if c not in T.cores and all(topo.may_write(c, d) for d in far)]
    ok.sort(key=lambda c: (topo.die(c) != topo.die(me), c))
    return ok[0], ok[1]


def view(T, name):
    return T[name][:].bitcast(dt.uint8) if SCRATCH[name][2] == X4 else T[name][:]


def write(g, T, topo, src, dst, out, in_, sem):
    rid, pid = topo.addr(dst, src)
    g.remote_dma(view(T, out), view(T, in_), T.sem[sem], T.sem.sent, pid, rid, topo.mask(src, dst))
    return len(topo.engines(src, dst))


def relay_program(g, core, T, topo, rank, kinds):
    me = T.cores[rank]
    n = 0
    for t in range(R):
        d = T.cores[rank ^ (1 << t)]
        for k in kinds:
            g.wait_ge(T.sem["a%s%d" % (k, t)], len(topo.engines(me, core)))
            n += write(g, T, topo, core, d, "far%s%d" % (k, t), "hop%s%d" % (k, t), "a%s%d" % (k, t))
    g.wait_ge(T.sem.sent, n)


def rank_program(g, core, T, topo):
    rank = T.rank_of(core)
    if rank is None:
        for r in range(len(T.cores)):
            a, b = relays(T, topo, r)
            if core == a:
                relay_program(g, core, T, topo, r, "pl")
            if core == b:
                relay_program(g, core, T, topo, r, "co")
        return
    ra, rb_ = relays(T, topo, rank)
    Q = {"v": g.vector, "a": g.scalar, "p": g.tensor, "g": g, "s": g.sync}
    SEM = {"v": "cv", "a": "ca", "p": "cp", "g": "cg"}
    count = {}
    seen = {}
    last_w = {}
    readers = {}

    def need(q, tok):
        if tok is not None and seen.get((q, tok[0]), 0) < tok[1]:
            Q[q].wait_ge(T.sem[tok[0]], tok[1])
            seen[(q, tok[0])] = tok[1]

    def order(q, rd, wr):
        toks = {}
        for tok in [last_w.get(k) for k in rd + wr] + [x for k in wr for x in readers.get(k, [])]:
            if tok is not None and not (q == "p" and tok[0] == "cp"):
                toks[tok[0]] = max(toks.get(tok[0], 0), tok[1])
        for s in sorted(toks):
            need(q, (s, toks[s]))

    def done(ins, sem, n, rd, wr):
        ins.then_inc(T.sem[sem], n)
        count[sem] = count.get(sem, 0) + n
        tok = (sem, count[sem])
        for k in wr:
            last_w[k] = tok
            readers[k] = []
        for k in rd:
            readers.setdefault(k, []).append(tok)

    def op(q, rd, wr, fn):
        wr = wr + [k for k in rd if k[:2] == "ps"]
        order(q, rd, wr)
        done(fn(), SEM[q], 1, rd, wr)

    def dma(q, sem, rd, wr, out, in_):
        order(q, rd, wr)
        done(Q[q].dma_start(out, in_), sem, 16, rd, wr)

    V, S, PE = g.vector, g.scalar, g.tensor

    def bank(b, n=C):
        return T.ps[:, 512 * b:512 * b + n]

    def part(name, b, n=C):
        return T[name][:, n * b:n * b + n]

    def four(name):
        return ["%s%d" % (name, b) for b in range(4)]

    def keys(name):
        return [name, name + "/0", name + "/1"]

    def mm(b, lq, lp, a, rq, rp, start=True, stop=True, h=None):
        lo, n = (0, C) if h is None else (128 * h, 128)
        rd = keys(rq) if h is None else [rq, "%s/%d" % (rq, h)]
        op("p", [lq, lp, rp] + rd, ["ps%d" % b], lambda: PE.matmul_mx(
            bank(b, n), T[lq][:, a:a + 128], T[lp][:, a:a + 128], T[rq][:, lo:lo + n], T[rp][:, lo:lo + n], start, stop))

    def quant(q, p, src, rd):
        op("v", rd, [q, p], lambda: V.quantize_mx(T[q][:], T[p][:], T[src][:]))

    def quant_half(q, p, src, rd, h):
        op("v", rd, ["%s/%d" % (q, h)], lambda: V.quantize_mx(part(q, h, 128), part(p, h, 128), part(src, h, 512)))

    def pick(q2, p2, q, p, key, off):
        op("v", keys(q) + [key], [q2], lambda: V.tensor_copy(T[q2][:].bitcast(dt.uint32), T[q][:].bitcast(dt.uint32).indirect(off)))
        op("a", keys(q) + [p, key], [p2], lambda: S.activation(T[p2][:], T[p][:].indirect(off), F.Copy))

    def wrap(name, mask="mdiag", out="cb"):
        op("v", [mask, name], [out], lambda: V.tensor_tensor_scan(T[out][:], T[mask][:], T[name][:, 0:C], 0.0, A.add, A.max))

    c0, c256, c1024, cfine, pm, pm16, pmh = (T.col[:, j:j + 1] for j in range(7))
    oi, oj, ok, om, ri, rj = T.oi[:, 0:16], T.oi[:, 16:32], T.oi[:, 32:40], T.oi[:, 40:48], T.oi[:, 48:56], T.oi[:, 56:64]
    ibi, ibj = T.ibi[:, 0:16], T.ibi[:, 16:32]

    def unwrap(key, out, ckey, s1, s2, op1, src="cb"):
        op("v", [src, ckey], [key], lambda: V.tensor_scalar(out, T[src][:, 15:C:16], s1, s2, A.add, op1))

    def signs(m):
        op("a", ["ps%d" % (2 + m)], ["sgo%d" % m], lambda: S.activation(T.sgo[:, m:768:3], bank(2 + m), F.Sign, bias=-ETA))

    def gather_a(out, okey, win, wkey, off):
        op("a", [wkey, off], [okey], lambda: S.activation(out, win.indirect(T[off][:]), F.Copy))

    def iota(key, pattern, base, out=None):
        op("g", [], [key], lambda: g.iota(T[key][:] if out is None else out, pattern, base, 0, allow_small_or_imprecise_dtypes=True))

    def line(key, out, rd, in_, scale, bias):
        op("a", [rd], [key], lambda: S.activation(out, in_, F.Identity, bias=bias, scale=scale))

    dma("s", "dx", [], ["xs"], T.xs[:], T.x[:])
    dma("a", "du", [], ["us"], T.us[:], T.u[:])
    op("v", [], ["one"], lambda: V.memset(T.one[:], 1.0))
    op("g", [], ["pi"], lambda: g.iota(T.ci[:, 32:40], [[0, 8]], 0, 1))
    op("g", [], ["uli"], lambda: g.iota(T.ci[:, 0:32], [[1, 4], [16, 8]], 0, 0))
    iota("row", [[0, 16], [1, 16]], 0)
    op("g", ["one"], ["ef"], lambda: g.affine_select(T.ef[:], T.one[:, 0:528], [[-1, 528]], A.is_equal, 0.0, 3, 4))
    iota("pay", [[1, C]], 0)
    op("v", ["pi"], ["pj"], lambda: V.tensor_scalar(T.ci[:, 40:48], T.ci[:, 32:40], 15, None, A.bitwise_and))
    op("v", ["uli"], ["ul"], lambda: V.tensor_copy(T.ul[:], T.ci[:, 0:32]))
    op("v", ["pj"], ["pm"], lambda: V.tensor_copy(pm, T.ci[:, 40:41]))
    op("v", [], ["mfz"], lambda: V.memset(T.mfar[:, 0:16], 0.0))
    line("pmh", pmh, "pm", pm, -1.0, -0.5)
    line("pm16", pm16, "pm", pm, 16.0, 0.0)
    line("c0", c0, "pm", pm, BIG, -15.0 * BIG)
    op("v", ["pm"], ["scz"], lambda: V.tensor_scalar(T.sc[:, 135:136], pm, 0.0, -1024.0, A.mult, A.add))
    op("v", ["row", "pm"], ["mown"], lambda: V.tensor_scalar(T.mown[:], T.row[:], pm, None, A.is_equal))
    op("v", ["row", "pm"], ["dl"], lambda: V.tensor_scalar(T.dl[:], T.row[:], pm, 4 * FAR, A.is_lt, A.mult))
    op("v", ["row"], ["keep"], lambda: V.tensor_scalar(T.keep[:], T.row[:], 0.0, None, A.is_gt))
    op("v", ["row", "pm16"], ["pl"], lambda: V.tensor_scalar(T.pl[:], T.row[:, 0:16], pm16, None, A.add))
    line("mfar", T.mfar[:, 16:272], "mown", T.mown[:], FAR, 0.0)
    op("a", ["row", "pmh"], ["msg"], lambda: S.activation(T.msg[:], T.row[:], F.Sign, bias=pmh))
    line("mdiag", T.mdiag[:], "msg", T.msg[:], (BIG + HUGE) / 2, (BIG - HUGE) / 2)
    line("mfine", T.mfine[:], "msg", T.msg[:], 132.0, -124.0)
    line("pos", T.pos[:], "pay", T.pay[:], FINE, -8.0)
    line("cfine", cfine, "pm", pm, 8.0, -108.0)
    op("v", ["mfar", "mfz"], ["t3"], lambda: V.tensor_tensor(T.t3[:], T.mfar[:, 15:271], T.mfar[:, 16:272], A.subtract))
    op("v", ["t3", "dl"], ["m3"], lambda: V.tensor_tensor(T.m3[:], T.dl[:], T.t3[:], A.add))
    quant("uq", "up", "us", ["us"])
    pick("u1q", "u1p", "uq", "up", "ul", T.ul[:, 0:8])
    quant("q0", "p0", "xs", ["xs"])
    pick("tc0", "tp0", "q0", "p0", "pl", T.pl[:])
    pick("u3q", "u3p", "uq", "up", "ul", T.ul[:, 8:32])
    sent = 0

    for t in range(R):
        buys = not rank >> t & 1
        last = t == R - 1
        tc, tp, ls, lt = "tc%d" % t, "tp%d" % t, "ls%d" % t, "lt%d" % t
        fc, fp, fl, fo_ = "farc%d" % t, "farp%d" % t, "farl%d" % t, "faro%d" % t
        partner = T.cores[rank ^ (1 << t)]
        for key, sem, relay in ((fc, "ac", rb_), (fp, "ap", ra), (fl, "al", ra), (fo_, "ao", rb_)):
            last_w[key] = ("%s%d" % (sem, t), len(topo.engines(relay, partner)))
        order("g", keys(tc), [])
        sent += write(g, T, topo, core, rb_, "hopc%d" % t, tc, "ac%d" % t)
        order("g", [tp], [])
        sent += write(g, T, topo, core, ra, "hopp%d" % t, tp, "ap%d" % t)
        if t == 0:
            op("g", ["one"], ["keep3"], lambda: g.affine_select(T.keep3[:], T.one[:, 0:768], [[0, C], [1, 3]], A.is_gt, 0.0, 0, 0))
            iota("step", [[0, C]], 13)
            iota("sto", [[0, 8]], 0, T.sto[:, 0:8])
        iota("wsg", [[0, 512]], 1)
        iota("wm", [[0, 1024]], 0)
        mm(0, "u1q", "u1p", 0, tc, tp)
        mm(1, "u1q", "u1p", 0, tc, tp)
        for m in range(3):
            mm(2 + m, "u3q", "u3p", 128 * m, tc, tp)
        way = A.add if buys else A.subtract
        own = T.hold[:, 15:C:16]
        op("v", ["ps0", "mown"], ["mk"], lambda: V.tensor_tensor(T.mk[:], bank(0), T.mown[:], A.mult))
        op("a", ["ps1"], ["dl"], lambda: S.activation(T.dl[:], bank(1), F.Abs, bias=ETA, scale=PHI if buys else -PHI))
        if t == 0:
            dma("s", "dwc", ["dl"], ["wq"], view(T, "wq"), T.wc[:])
            dma("s", "dws", [], ["wp"], T.wp[:], T.ws[:])
            dma("s", "dv", [], ["vs"], T.vs[:], T.v[:])
        signs(0)
        op("v", ["mk", "keep"], ["hold"], lambda: V.tensor_tensor_scan(T.hold[:], T.keep[:], T.mk[:], 0.0, A.mult, way))
        op("v", ["dl", "m3"], ["t3"], lambda: V.tensor_tensor_scan(T.t3[:], T.m3[:], T.dl[:], 0.0, A.add, A.min))
        op("a", ["hold"], ["dw"], lambda: S.activation(T.dw[:], own, F.Abs, bias=ETA, scale=PHI))
        op("a", ["hold"], ["rb0"], lambda: S.activation(T.rb[:, 0:16], own, F.Copy))
        op("v", ["t3", "ps0"], ["rb1"], lambda: V.tensor_tensor(T.rb[:, 16:272], T.t3[:], bank(0), way))
        op("v", ["hold", "dw"], ["rb2"], lambda: V.tensor_tensor(T.rb[:, 272:288], own, T.dw[:], A.add))
        signs(1)
        signs(2)
        rbs = ["rb0", "rb1", "rb2"]
        for k in range(ND):
            op("v", rbs, ["cm%d" % k], lambda: V.tensor_scalar(part("cm", k, 272), T.rb[:, k:k + 272], T.rb[:, k:k + 1], None, A.is_gt))
        for k in range(ND, 16):
            op("a", rbs, ["sa%d" % k], lambda: S.activation(
                part("sa", k - ND, 272), T.rb[:, k:k + 272], F.Sign, bias=T.rb[:, k:k + 1], scale=-1.0))
        for k in range(ND, 16):
            op("a", ["sa%d" % k], ["sa%d" % k, "rk%d" % k], lambda: S.activation(
                part("sa", k - ND, 272), part("sa", k - ND, 272), F.Relu, scale=-1.0, accum_out=T.rk[:, k:k + 1]))
        op("v", ["cm%d" % k for k in range(ND)], ["sc"], lambda: V.tensor_tensor_scan(
            T.sc[:, 136:], T.cm[:, 0:272 * ND:2], T.cm[:, 1:272 * ND:2], -1024.0, A.add, A.add))
        if t == 0:
            line("c256", c256, "c0", c0, 1.0, 256.0)
            line("c1024", c1024, "c0", c0, 1.0, -1024.0)
        op("v", ["sgo0", "sgo1", "sgo2", "keep3"], ["vv"], lambda: V.tensor_tensor_scan(T.vv[:], T.keep3[:], T.sgo[:], 0.0, A.mult, A.add))
        op("v", ["sc", "scz"], ["rkv"], lambda: V.tensor_tensor(
            T.rk[:, 0:ND], T.sc[:, 271:136 * ND + 136:136], T.sc[:, 135:136 * ND:136], A.subtract))
        op("v", ["vv", "pos"], ["pay"], lambda: V.tensor_tensor_scan(T.pay[:], T.vv[:, 2:768:3], T.pos[:], -8.0, A.max, A.add))
        if t == 0:
            for b in range(4):
                op("v", ["ef"], ["eq", "ep"] if b == 3 else ["eq%d" % b], lambda: V.quantize_mx(
                    part("eq", b, 128), part("ep", b, 128), T.ef[:, 3 - b:515 - b]))
        op("v", ["rkv"] + ["rk%d" % k for k in range(ND, 16)], ["rko"], lambda: V.tensor_copy(T.rko[:], T.rk[:]))
        op("v", ["pay", "rko"], ["vsd"], lambda: V.tensor_copy(T.vsd[:].indirect(T.rko[:]), T.pay[:]))
        op("v", ["vsd", "step"], ["sto"], lambda: V.tensor_tensor_scan(T.sto[:, 1:C + 1], T.vsd[:], T.step[:], 0.0, A.add, A.add))
        wrap("vsd", "mfine", "cb2")
        wrap("sto")
        unwrap("oi", oi, "cfine", cfine, 1.0 / FINE, A.mult, "cb2")
        unwrap(ls, T[ls][:], "c0", c0, 0.5, A.mult)
        order("g", [ls], [])
        sent += write(g, T, topo, core, ra, "hopl%d" % t, ls, "al%d" % t)
        for b in range(4):
            mm(b, "eq", "ep", 128 * b, tc, tp)
        for b in range(4):
            mm(4 + b, "eq", "ep", 128 * b, fc, fp)
        for b in range(4):
            op("a", ["ps%d" % b], ["do%d" % b], lambda: S.activation(part("do", b), bank(b), F.Copy, scale=0.5))
        for b in range(4):
            op("a", ["ps%d" % (4 + b)], ["dp%d" % b], lambda: S.activation(part("dp", b), bank(4 + b), F.Copy, scale=0.5))
        op("v", ["oi"], ["oj"], lambda: V.tensor_scalar(oj, oi, 255, None, A.bitwise_and))
        op("v", ["oj"], ["lo"], lambda: V.tensor_copy(T.lo[:], oj))
        for b in range(4):
            gather_a(part("dos", b), "dos%d" % b, part("do", b), "do%d" % b, "lo")
        op("v", ["oj"], ["ok"], lambda: V.tensor_scalar(ok, T.oi[:, 16:24], 256.0, None, A.mult))
        op("v", ["oj", "ok"], ["om"], lambda: V.tensor_tensor(om, ok, T.oi[:, 24:32], A.add))
        op("v", ["om"], [lt], lambda: V.tensor_copy(T[lt][:], om))
        order("g", [lt], [])
        sent += write(g, T, topo, core, rb_, "hopo%d" % t, lt, "ao%d" % t)
        if t == 0:
            iota("hsz", [[0, 4]], 0, T.hs[:, C:272 * 4:272])
        op("v", ["one", ls], ["wm"], lambda: V.tensor_copy(T.wm[:].indirect(T[ls][:]), T.one[:, 0:C]))
        op("v", ["wm"], ["wm2"], lambda: V.tensor_copy(T.wm2[:], T.wm[:]))
        if t == 1:
            iota("ft", [[1, 272]], 0)
            iota("ft", [[0, 8]], -1, T.ft[:, C:C + 8])
            quant("vq", "vp", "vs", ["vs"])
        if last:
            pick("nq", "np", tc, tp, "pl", T.pl[:])
        dq, dp_ = ("nq", "np") if last else (tc, tp)
        for b in range(4):
            mm(b, "eq", "ep", 128 * b, dq, dp_, True, False, 0)
        op("v", ["one", fl], ["wm"], lambda: V.tensor_copy(T.wm[:].indirect(T[fl][:]), T.one[:, 0:C]))
        op("a", ["wm2", fl], ["bv"], lambda: S.activation(T.bv[:], T.wm2[:].indirect(T[fl][:]), F.Identity, bias=1024.0))
        op("v", ["wm", "one"], ["seg"], lambda: V.tensor_tensor_scan(T.seg[:], T.one[:], T.wm[:], -257.0, A.mult, A.add))
        op("v", [fo_], ["ri"], lambda: V.tensor_copy(ri, T[fo_][:]))
        op("v", ["seg", fl, "mown"], ["fpr"], lambda: V.tensor_tensor(T.fpr[:], T.seg[:].indirect(T[fl][:]), T.mown[:], A.mult))
        gather_a(T.fsr[:], "fsr", T.seg[:], "seg", ls)
        gather_a(T.fow[:], "fow", T.fsr[:], "fsr", "rko")
        if last:
            gather_a(T.fna[:], "fna", T.fow[:], "fow", "pl")
        op("v", ["ri"], ["rj"], lambda: V.tensor_scalar(rj, ri, 255, None, A.bitwise_and))
        op("v", ["fpr", "keep"], ["cbh"], lambda: V.tensor_tensor_scan(T.cbh[:], T.keep[:], T.fpr[:], 0.0, A.mult, A.add))
        op("v", [fo_], ["lp0"], lambda: V.tensor_scalar(T.lp[:, 0:8], T[fo_][:], 1.0 / 256, -0.498046875, A.mult, A.add))
        op("v", ["cbh"], ["fpo"], lambda: V.tensor_scalar(T.fpo[:], T.cbh[:, 15:C:16], 256.0, None, A.add))
        op("v", ["rj", "lp0"], ["lp"], lambda: V.tensor_copy(T.lp[:, 8:16], rj))
        for b in range(4):
            gather_a(part("dps", b), "dps%d" % b, part("dp", b), "dp%d" % b, "lp")
        op("v", ["bv", "fpo"], ["wsg"], lambda: V.tensor_copy(T.wsg[:].indirect(T.fpo[:]), T.bv[:]))
        op("v", ["wsg"], ["cum"], lambda: V.tensor_tensor_scan(T.cum[:], T.wsg[:, 0:C], T.wsg[:, 0:C], 0.0, A.add, A.max))
        wrap("cum")
        unwrap("ia", T.ia[:], "c1024", c1024, 1.0 / 1024, A.mult)
        unwrap("ibi", ibi, "c0", c0, -1.0, A.add)
        op("v", ["ibi"], ["ibj"], lambda: V.tensor_scalar(ibj, ibi, 1023, None, A.bitwise_and))
        op("v", ["ibj"], ["ib"], lambda: V.tensor_copy(T.ib[:], ibj))
        for b in range(4):
            gather_a(part("tmp", b), "tmp%d" % b, part("dps", b), "dps%d" % b, "ia")
            op("v", ["dos%d" % b, "ib", "tmp%d" % b], ["z%d" % b], lambda: V.tensor_tensor(
                T.z[:, b:1024:4], part("dos", b).indirect(T.ib[:]), part("tmp", b), A.add))
        quant("zq", "zp", "z", four("z"))
        for b in range(4):
            mm(4 + b, "wq", "wp", 128 * b, "zq", "zp")
        wrap("fna" if last else "fow")
        unwrap("fo", T.fo[:], "c256", c256, 256.0, A.min)
        for b in (0, 2):
            op("a", ["ps%d" % (4 + b), "hsz"], ["hs%d" % b], lambda: S.activation(T.hs[:, 272 * b:272 * b + C], bank(4 + b), F.Relu, scale=0.03125))
        for b in (1, 3):
            op("v", ["ps%d" % (4 + b), "hsz"], ["hs%d" % b], lambda: V.tensor_scalar(T.hs[:, 272 * b:272 * b + C], bank(4 + b), 0.0, 0.03125, A.max, A.mult))
        for b in range(4):
            mm(4 + b, "eq", "ep", 128 * b, dq, dp_, True, False, 1)
        nq, np_ = "tc%d" % (t + 1), "tp%d" % (t + 1)

        def bring(q, b, h):
            out, win, off = T.hg[:, 512 * h + b:512 * h + 512:4], T.hs[:, 272 * b:272 * b + C + 1], T.fo[:, 8 * h:8 * h + 8]
            op(q, ["hs%d" % b, "fo"], ["hg%d%d" % (b, h)], (lambda: V.tensor_copy(out, win.indirect(off))) if q == "v" else (
                lambda: S.activation(out, win.indirect(off), F.Copy)))

        def fetch(q, key, out, b):
            op(q, ["ps%d" % b], [key], (lambda: V.tensor_copy(out, bank(b, 128))) if q == "v" else (
                lambda: S.activation(out, bank(b, 128), F.Copy)))

        for h in range(2):
            for q, b in BRING[h]:
                bring(q, b, h)
            quant_half("hq", "hp", "hg", ["hg%d%d" % (b, h) for b in range(4)], h)
            for b in range(4):
                mm(4 * h + b, "eq", "ep", 128 * b, "hq", "hp", False, True, h)
        for h in range(2):
            for q, b in FETCH[h]:
                fetch(q, "xn%d%d" % (b, h), T.xn[:, 512 * h + b:512 * h + 512:4], 4 * h + b)
            quant_half(nq, np_, "xn", ["xn%d%d" % (b, h) for b in range(4)], h)
            if last:
                mm(4 * h, "vq", "vp", 0, nq, np_, True, True, h)
                dma("s", "dout", ["%s/%d" % (nq, h)], [], part("oc", h, 512), part(nq, h, 128).bitcast(dt.uint8))

    tc, tp = "tc%d" % R, "tp%d" % R
    fetch("a", "ys0", part("ys", 0, 128), 0)
    dma("s", "dout", ["ys0"], [], part("y", 0, 128), part("ys", 0, 128))
    gather_a(T.olr[:], "olr", T.ft[:], "ft", "fo")
    fetch("v", "ys1", part("ys", 1, 128), 4)
    dma("s", "dout", ["ys1"], [], part("y", 1, 128), part("ys", 1, 128))
    dma("a", "dout", ["olr"], [], T.ol[:], T.olr[0:128:16, :])
    for k in range(4):
        dma("a", "dout", keys(tc), [], T.osc[4 * k:4 * k + 4, :], T[tp][32 * k:32 * k + 4, :])
    g.wait_ge(T.sem.sent, sent)
    for s in sorted(count):
        need("g", (s, count[s]))
